import numpy as np
import ml_dtypes


def mxq(x, axis, fmt="e4m3"):
    dtype, down = {"e4m3": (ml_dtypes.float8_e4m3fn, 7), "e5m2": (ml_dtypes.float8_e5m2, 14)}[fmt]
    v = np.moveaxis(np.asarray(x, np.float32).astype(ml_dtypes.bfloat16).astype(np.float64), axis, -1)
    blocks = v.reshape(v.shape[:-1] + (-1, 32))
    amax = np.abs(blocks).max(-1, keepdims=True)
    byte = np.maximum(np.where(amax > 0, np.frexp(amax)[1] - 1 + 127, 0) - down, 1)
    scale = np.exp2(byte - 127.0)
    codes = (blocks / scale).astype(np.float32).astype(dtype).astype(np.float64)
    return np.moveaxis((codes * scale).reshape(v.shape), -1, axis)


WIDE = False


def mx_kscale(k):
    if not WIDE:
        return np.ones(k)
    levels = np.array([10, -10, 5, -5, 0])
    if k % 512:
        return np.exp2(np.random.permutation(np.resize(levels, k // 32))).repeat(32)
    a = np.empty((k // 512, 16))
    for p in range(k // 512):
        a[p, :8] = np.random.permutation(np.resize(levels, 8))
        for g in range(8):
            far = levels[np.abs(levels - a[p, g]) >= 10]
            a[p, g + 8] = far[np.random.randint(len(far))]
    return np.exp2(a.ravel()).repeat(32)


def f64(x):
    return np.asarray(x).astype(np.float64)


def striped(idx):
    return np.tile(idx.reshape(-1, 16).T, (8, 1)).astype(np.uint16)


def unstriped(offs):
    return offs[:16].T.reshape(-1).astype(np.int64)


E2M1 = np.array([0.0, 0.5, 1.0, 1.5, 2.0, 3.0, 4.0, 6.0, -0.0, -0.5, -1.0, -1.5, -2.0, -3.0, -4.0, -6.0])


def pack_fp4(w):
    k, n = w.shape
    w = f64(np.asarray(w, np.float32).astype(ml_dtypes.bfloat16)).reshape(k // 32, 32, n)
    amax = np.abs(w).max(1)
    mant, ex = np.frexp(amax / 6.0)
    byte = np.clip(np.where(amax > 0, np.where(mant > 0.5, ex, ex - 1) + 127, 1), 1, 254)
    scaled = (w * np.exp2(127.0 - byte)[:, None, :]).reshape(k, n).astype(np.float32)
    c = np.ascontiguousarray(scaled.reshape(k // 512, 128, 4, n).transpose(0, 1, 3, 2)).astype(ml_dtypes.float4_e2m1fn).view(np.uint8) & 0xF
    words = (c[..., 0::2] | (c[..., 1::2] << 4)).reshape(k // 512, 128, 2 * n)
    return np.ascontiguousarray(words), np.ascontiguousarray(byte.astype(np.uint8).reshape(k // 512, 16, n))


def unpack_fp4(words, scales):
    g, _, n = scales.shape
    words = np.ascontiguousarray(words).reshape(g, 128, n, 2)
    nib = np.empty((g, 128, n, 4), np.uint8)
    nib[..., 0::2] = words & 0xF
    nib[..., 1::2] = words >> 4
    vals = E2M1[nib] * np.repeat(np.exp2(scales.astype(np.float64) - 127.0), 8, axis=1)[..., None]
    return vals.transpose(0, 1, 3, 2).reshape(g * 512, n)


def gelu(v):
    return 0.5 * v * (1.0 + np.tanh(np.sqrt(2.0 / np.pi) * (v + 0.044715 * v**3)))


K, T, S, V, N = 512, 4096, 1024, 512, 256


def setup_inputs():
    n = np.random.standard_normal
    s = mx_kscale(K)[:, None]
    packed_w1 = pack_fp4(n((K, N)) / np.sqrt(K) / s)
    return {
        "xT": (n((K, T)) * s).astype(np.float32),
        "w1_words": packed_w1[0],
        "w1_scales": packed_w1[1],
        "offs": striped(np.random.permutation(T)[:S]),
        "pos1": striped(np.random.permutation(S)[:V]),
        "pos2": striped(np.random.permutation(S)[:V]),
        "pos3": striped(np.random.permutation(S)[:V]),
    }


def reference(xT, w1_words, w1_scales, offs, pos1, pos2, pos3):
    xq = mxq(f64(xT)[:, unstriped(offs)], 0, "e4m3")
    y = gelu(unpack_fp4(w1_words, w1_scales).T @ xq)
    n0 = y[:, unstriped(pos1)]
    n1 = y[:, unstriped(pos2)]
    n2 = y[:, unstriped(pos3)]
    return np.maximum(np.minimum(n0, n1), np.minimum(np.maximum(n0, n1), n2))

@@ -1,0 +1,156 @@
+from contextlib import ExitStack
+
+import concourse.mybir as mybir
+
+K, T, S, V, N = 512, 4096, 1024, 512, 256
+FLOPS = 2 * K * N * S
+
+F32 = mybir.dt.float32
+BF16 = mybir.dt.bfloat16
+I32 = mybir.dt.int32
+U32 = mybir.dt.uint32
+U16 = mybir.dt.uint16
+U8 = mybir.dt.uint8
+FP8X4 = mybir.dt.float8_e4m3fn_x4
+FP4X4 = mybir.dt.float4_e2m1fn_x4
+ALU = mybir.AluOpType
+ACT = mybir.ActivationFunctionType
+
+P = 128
+PACK = 4
+HALF = S // 2
+PIECE = 256
+SHARE = True
+FUSED = True
+WARM = True
+CHUNKS = [[1024,"s"],[1024,"s"],[1024,"v"],[768,"v"],[256,"s"]]
+
+
+def tile_picked_median_gelu_e_kernel(
+    tc, xT, w1_words, w1_scales, offs, pos1, pos2, pos3, out
+):
+    nc = tc.nc
+    with ExitStack() as ctx:
+        keep = ctx.enter_context(tc.tile_pool(name="keep", bufs=1))
+        psum = ctx.enter_context(tc.psum_pool(name="psum", bufs=1))
+
+        rows = xT.rearrange("(p j) t -> p j t", j=PACK)
+        planes = [keep.tile([P, T], F32, name=f"plane{j}") for j in range(PACK)]
+        picks = keep.tile([P, S // 16], U16, name="picks")
+        places = [keep.tile([P, V // 16], U16, name=f"places{d}") for d in range(3)]
+        w_words = keep.tile([P, 2 * N], U8, name="w_words", align_bytes=64)
+        w_scales = keep.tile([P, N], U8, name="w_scales", align_bytes=64)
+        grouped = [keep.tile([P, HALF, PACK], BF16, name=f"grouped{h}", align_bytes=64) for h in range(2)]
+        codes = keep.tile([P, S], U32, name="codes", align_bytes=64)
+        scales = keep.tile([P, S], U8, name="scales", align_bytes=64)
+        y = [keep.tile([P, S], F32, name=f"y{m}") for m in range(2)]
+
+        order = [2, 0, 1, 3] if SHARE else [0, 1, 2, 3]
+        if WARM:
+            warm = keep.tile([P, 2], F32, name="warm")
+            nc.vector.memset(warm[:, 0:1], 0.0)
+            nc.scalar.activation(warm[:, 1:2], warm[:, 0:1], ACT.Gelu_apprx_tanh)
+
+        nc.gpsimd.memset(w_scales[:].bitcast(I32), 0)
+        nc.gpsimd.dma_start(out=w_words[:].bitcast(I32), in_=w1_words[0].bitcast(I32))
+        for q in range(4):
+            nc.gpsimd.dma_start(
+                out=w_scales[32 * q : 32 * q + 4, :].bitcast(I32),
+                in_=w1_scales[0, 4 * q : 4 * q + 4, :].bitcast(I32),
+            )
+
+        def pick(h):
+            return picks[:, h * (HALF // 16) : (h + 1) * (HALF // 16)]
+
+        def vgather(j, h):
+            nc.vector.tensor_copy(grouped[h][:, :, j], planes[j][:].indirect(pick(h)))
+
+        halves = {}
+        if SHARE:
+            for j in (2, 3):
+                halves[j] = keep.tile([P, T], BF16, name=f"rounded{j}")
+
+        def sgather(j):
+            nc.scalar.activation(grouped[1][:, :, j], halves[j][:].indirect(pick(1)), ACT.Copy)
+
+        for i, j in enumerate(order):
+            if SHARE and j == 3:
+                c0 = 0
+                for w, e in CHUNKS:
+                    nc.sync.dma_start(out=planes[j][:, c0 : c0 + w], in_=rows[:, j, c0 : c0 + w])
+                    if e == "s":
+                        nc.scalar.copy(halves[j][:, c0 : c0 + w], planes[j][:, c0 : c0 + w])
+                    else:
+                        nc.vector.tensor_copy(halves[j][:, c0 : c0 + w], planes[j][:, c0 : c0 + w])
+                    c0 = c0 + w
+            else:
+                nc.sync.dma_start(out=planes[j][:], in_=rows[:, j, :])
+            if i == 0:
+                nc.sync.dma_start(picks[:], offs)
+            if i == 1:
+                for d, src in enumerate((pos1, pos2, pos3)):
+                    nc.sync.dma_start(places[d][:], src)
+            if SHARE and j == 2:
+                nc.scalar.copy(halves[j][:], planes[j][:])
+            vgather(j, 0)
+            if SHARE and j >= 2:
+                sgather(j)
+            else:
+                vgather(j, 1)
+
+        npiece = S // PIECE
+        per_half = HALF // PIECE
+
+        def product(m, c0, width, tag):
+            acc = psum.tile([P, 512], F32, name=tag, tag=tag)
+            nc.tensor.matmul_mx(
+                out=acc[:, 0:width],
+                lhsT=w_words[:, 2 * P * m : 2 * P * (m + 1)].bitcast(FP4X4),
+                lhsT_scale=w_scales[:, P * m : P * (m + 1)],
+                rhs=codes[:, c0 : c0 + width].bitcast(FP8X4),
+                rhs_scale=scales[:, c0 : c0 + width],
+                start=True,
+                stop=True,
+            )
+            nc.scalar.activation(y[m][:, c0 : c0 + width], acc[:, 0:width], ACT.Gelu_apprx_tanh)
+
+        for i in range(npiece):
+            h, r = divmod(i, per_half)
+            c0 = i * PIECE
+            nc.vector.quantize_mx(
+                out=codes[:, c0 : c0 + PIECE].bitcast(FP8X4),
+                scales=scales[:, c0 : c0 + PIECE],
+                in_=grouped[h][:, r * PIECE : (r + 1) * PIECE, :].rearrange("p s j -> p (s j)"),
+            )
+            product(0, c0, PIECE, f"acc{i}")
+        for h in range(2):
+            product(1, h * HALF, HALF, f"acc{npiece - 1 - h}")
+
+        for m in range(2):
+            gtags = [["b0", "p0", "q0"], ["b1", "q0", "t0"]][m]
+            ttags = [["t0", "u0", "w0"], ["b0", "u1", "w1"]][m]
+            g = [keep.tile([P, V], F32, name=f"g{m}_{d}", tag=gtags[d]) for d in range(3)]
+            t = [keep.tile([P, V], F32, name=f"t{m}_{d}", tag=ttags[d]) for d in range(2 if FUSED else 3)]
+            res = keep.tile([P, V], F32, name=f"res{m}")
+            parts = [(0, V)] if m == 0 else [(0, V // 2), (V // 2, V)]
+            if FUSED:
+                nc.vector.tensor_copy(g[0][:], y[m][:].indirect(places[0][:]))
+                for d in (1, 2):
+                    nc.vector.tensor_tensor(g[d][:], y[m][:].indirect(places[d][:]), g[0][:], ALU.subtract)
+                for a, b in parts:
+                    nc.vector.scalar_tensor_tensor(t[0][:, a:b], g[1][:, a:b], 0.0, g[2][:, a:b], ALU.max, ALU.min)
+                for a, b in parts:
+                    nc.vector.scalar_tensor_tensor(t[1][:, a:b], g[1][:, a:b], 0.0, t[0][:, a:b], ALU.min, ALU.max)
+                for a, b in parts:
+                    nc.vector.tensor_tensor(res[:, a:b], t[1][:, a:b], g[0][:, a:b], ALU.add)
+                    nc.sync.dma_start(out=out[m * P : (m + 1) * P, a:b], in_=res[:, a:b])
+            else:
+                for d in range(3):
+                    nc.vector.tensor_copy(g[d][:], y[m][:].indirect(places[d][:]))
+                nc.vector.tensor_tensor(t[0][:], g[0][:], g[1][:], ALU.max)
+                nc.vector.tensor_tensor(t[1][:], g[0][:], g[1][:], ALU.min)
+                for a, b in parts:
+                    nc.vector.tensor_tensor(t[2][:, a:b], t[0][:, a:b], g[2][:, a:b], ALU.min)
+                for a, b in parts:
+                    nc.vector.tensor_tensor(res[:, a:b], t[1][:, a:b], t[2][:, a:b], ALU.max)
+                    nc.sync.dma_start(out=out[m * P : (m + 1) * P, a:b], in_=res[:, a:b])

@@ -19,9 +19,9 @@ ACT = mybir.ActivationFunctionType
 P = 128
 PACK = 4
 HALF = S // 2
-PIECE = 256
+PIECES = [256,256,256,128,128]
 SHARE = True
-FUSED = True
+FUSED = False
 WARM = True
 CHUNKS = [[1024,"s"],[1024,"s"],[1024,"v"],[768,"v"],[256,"s"]]
 
@@ -52,12 +52,6 @@ def tile_picked_median_gelu_e_kernel(
             nc.scalar.activation(warm[:, 1:2], warm[:, 0:1], ACT.Gelu_apprx_tanh)
 
         nc.gpsimd.memset(w_scales[:].bitcast(I32), 0)
-        nc.gpsimd.dma_start(out=w_words[:].bitcast(I32), in_=w1_words[0].bitcast(I32))
-        for q in range(4):
-            nc.gpsimd.dma_start(
-                out=w_scales[32 * q : 32 * q + 4, :].bitcast(I32),
-                in_=w1_scales[0, 4 * q : 4 * q + 4, :].bitcast(I32),
-            )
 
         def pick(h):
             return picks[:, h * (HALF // 16) : (h + 1) * (HALF // 16)]
@@ -87,7 +81,13 @@ def tile_picked_median_gelu_e_kernel(
                 nc.sync.dma_start(out=planes[j][:], in_=rows[:, j, :])
             if i == 0:
                 nc.sync.dma_start(picks[:], offs)
-            if i == 1:
+            if i == 3:
+                nc.sync.dma_start(out=w_words[:].bitcast(I32), in_=w1_words[0].bitcast(I32))
+                for q in range(4):
+                    nc.sync.dma_start(
+                        out=w_scales[32 * q : 32 * q + 4, :].bitcast(I32),
+                        in_=w1_scales[0, 4 * q : 4 * q + 4, :].bitcast(I32),
+                    )
                 for d, src in enumerate((pos1, pos2, pos3)):
                     nc.sync.dma_start(places[d][:], src)
             if SHARE and j == 2:
@@ -98,8 +98,6 @@ def tile_picked_median_gelu_e_kernel(
             else:
                 vgather(j, 1)
 
-        npiece = S // PIECE
-        per_half = HALF // PIECE
 
         def product(m, c0, width, tag):
             acc = psum.tile([P, 512], F32, name=tag, tag=tag)
@@ -114,23 +112,22 @@ def tile_picked_median_gelu_e_kernel(
             )
             nc.scalar.activation(y[m][:, c0 : c0 + width], acc[:, 0:width], ACT.Gelu_apprx_tanh)
 
-        for i in range(npiece):
-            h, r = divmod(i, per_half)
-            c0 = i * PIECE
+        c0 = 0
+        for i, w in enumerate(PIECES):
+            h, r = divmod(c0, HALF)
             nc.vector.quantize_mx(
-                out=codes[:, c0 : c0 + PIECE].bitcast(FP8X4),
-                scales=scales[:, c0 : c0 + PIECE],
-                in_=grouped[h][:, r * PIECE : (r + 1) * PIECE, :].rearrange("p s j -> p (s j)"),
+                out=codes[:, c0 : c0 + w].bitcast(FP8X4),
+                scales=scales[:, c0 : c0 + w],
+                in_=grouped[h][:, r : r + w, :].rearrange("p s j -> p (s j)"),
             )
-            product(0, c0, PIECE, f"acc{i}")
+            product(0, c0, w, f"acc{i}")
+            c0 = c0 + w
         for h in range(2):
-            product(1, h * HALF, HALF, f"acc{npiece - 1 - h}")
+            product(1, h * HALF, HALF, f"acc{len(PIECES) - 1 - h}")
 
         for m in range(2):
-            gtags = [["b0", "p0", "q0"], ["b1", "q0", "t0"]][m]
-            ttags = [["t0", "u0", "w0"], ["b0", "u1", "w1"]][m]
-            g = [keep.tile([P, V], F32, name=f"g{m}_{d}", tag=gtags[d]) for d in range(3)]
-            t = [keep.tile([P, V], F32, name=f"t{m}_{d}", tag=ttags[d]) for d in range(2 if FUSED else 3)]
+            g = [keep.tile([P, V], F32, name=f"g{m}_{d}") for d in range(3)]
+            t = [keep.tile([P, V], F32, name=f"t{m}_{d}") for d in range(3)]
             res = keep.tile([P, V], F32, name=f"res{m}")
             parts = [(0, V)] if m == 0 else [(0, V // 2), (V // 2, V)]
             if FUSED:

@@ -1,6 +1,7 @@
 from contextlib import ExitStack
 
 import concourse.mybir as mybir
+from concourse.masks import make_identity
 
 K, T, S, V, N = 512, 4096, 1024, 512, 256
 FLOPS = 2 * K * N * S
@@ -21,9 +22,9 @@ PACK = 4
 HALF = S // 2
 PIECES = [256,256,256,128,128]
 SHARE = True
-FUSED = False
+FUSED = True
 WARM = True
-CHUNKS = [[1024,"s"],[1024,"s"],[1024,"v"],[768,"v"],[256,"s"]]
+CHUNKS = [[1024,1024],[1024,1024],[1024,512],[768,0],[256,256]]
 
 
 def tile_picked_median_gelu_e_kernel(
@@ -53,6 +54,9 @@ def tile_picked_median_gelu_e_kernel(
 
         nc.gpsimd.memset(w_scales[:].bitcast(I32), 0)
 
+        ident = keep.tile([P, P], F32, name="ident")
+        make_identity(nc, ident[:])
+
         def pick(h):
             return picks[:, h * (HALF // 16) : (h + 1) * (HALF // 16)]
 
@@ -70,12 +74,12 @@ def tile_picked_median_gelu_e_kernel(
         for i, j in enumerate(order):
             if SHARE and j == 3:
                 c0 = 0
-                for w, e in CHUNKS:
+                for w, ws in CHUNKS:
                     nc.sync.dma_start(out=planes[j][:, c0 : c0 + w], in_=rows[:, j, c0 : c0 + w])
-                    if e == "s":
-                        nc.scalar.copy(halves[j][:, c0 : c0 + w], planes[j][:, c0 : c0 + w])
-                    else:
-                        nc.vector.tensor_copy(halves[j][:, c0 : c0 + w], planes[j][:, c0 : c0 + w])
+                    if ws > 0:
+                        nc.scalar.copy(halves[j][:, c0 : c0 + ws], planes[j][:, c0 : c0 + ws])
+                    if ws < w:
+                        nc.vector.tensor_copy(halves[j][:, c0 + ws : c0 + w], planes[j][:, c0 + ws : c0 + w])
                     c0 = c0 + w
             else:
                 nc.sync.dma_start(out=planes[j][:], in_=rows[:, j, :])
@@ -125,29 +129,55 @@ def tile_picked_median_gelu_e_kernel(
         for h in range(2):
             product(1, h * HALF, HALF, f"acc{len(PIECES) - 1 - h}")
 
+        def fetch(m, d, a, b):
+            return y[m][:].indirect(places[d][:, a // 16 : b // 16])
+
+        def turned_sum(bank, first, second, c0, width):
+            for c in range(0, width, P):
+                for i, src in enumerate((first, second)):
+                    nc.tensor.matmul(
+                        bank[:, c : c + P], lhsT=src[:, c0 + c : c0 + c + P], rhs=ident[:],
+                        is_transpose=True, start=(i == 0), stop=(i == 1),
+                    )
+
+        parts = [(0, V // 2), (V // 2, V)]
         for m in range(2):
-            g = [keep.tile([P, V], F32, name=f"g{m}_{d}") for d in range(3)]
-            t = [keep.tile([P, V], F32, name=f"t{m}_{d}") for d in range(3)]
+            base = keep.tile([P, V], F32, name=f"base{m}")
+            p = keep.tile([P, V], F32, name=f"p{m}")
+            q = keep.tile([P, V], F32, name=f"q{m}")
+            t = keep.tile([P, V], F32, name=f"t{m}")
             res = keep.tile([P, V], F32, name=f"res{m}")
-            parts = [(0, V)] if m == 0 else [(0, V // 2), (V // 2, V)]
-            if FUSED:
-                nc.vector.tensor_copy(g[0][:], y[m][:].indirect(places[0][:]))
-                for d in (1, 2):
-                    nc.vector.tensor_tensor(g[d][:], y[m][:].indirect(places[d][:]), g[0][:], ALU.subtract)
-                for a, b in parts:
-                    nc.vector.scalar_tensor_tensor(t[0][:, a:b], g[1][:, a:b], 0.0, g[2][:, a:b], ALU.max, ALU.min)
-                for a, b in parts:
-                    nc.vector.scalar_tensor_tensor(t[1][:, a:b], g[1][:, a:b], 0.0, t[0][:, a:b], ALU.min, ALU.max)
-                for a, b in parts:
-                    nc.vector.tensor_tensor(res[:, a:b], t[1][:, a:b], g[0][:, a:b], ALU.add)
-                    nc.sync.dma_start(out=out[m * P : (m + 1) * P, a:b], in_=res[:, a:b])
+            for a, b in (parts if m == 0 else [(0, V)]):
+                nc.vector.tensor_copy(base[:, a:b], fetch(m, 0, a, b))
+            for a, b in (parts if m == 0 else [(0, V)]):
+                nc.vector.tensor_tensor(p[:, a:b], fetch(m, 1, a, b), base[:, a:b], ALU.subtract)
+            for a, b in (parts if m == 0 else [(0, V)]):
+                nc.vector.tensor_tensor(q[:, a:b], fetch(m, 2, a, b), base[:, a:b], ALU.subtract)
+            for a, b in parts:
+                nc.vector.scalar_tensor_tensor(t[:, a:b], p[:, a:b], 0.0, q[:, a:b], ALU.max, ALU.min)
+            if m == 0:
+                nb = keep.tile([P, V], F32, name="nb")
+                n = keep.tile([P, V], F32, name="n")
+                low_t = keep.tile([P, V], F32, name="low_t")
+                rise_t = keep.tile([P, V], F32, name="rise_t")
+                nc.scalar.activation(nb[:], base[:], ACT.Copy, scale=-1.0)
+                nc.scalar.activation(n[:], p[:], ACT.Relu, scale=-1.0)
+                lbank = psum.tile([P, 512], F32, name="lbank", tag="lbank")
+                turned_sum(lbank, nb, n, 0, V)
+                nc.scalar.activation(low_t[:], lbank[:], ACT.Copy, scale=-1.0)
+                for i, (a, b) in enumerate(parts):
+                    ubank = psum.tile([P, 512], F32, name=f"ubank{i}", tag=f"ubank{i}")
+                    turned_sum(ubank, n, t, a, b - a)
+                    nc.scalar.activation(rise_t[:, a:b], ubank[:, 0 : b - a], ACT.Relu)
+                for i, (a, b) in enumerate(parts):
+                    obank = psum.tile([P, 512], F32, name=f"obank{i}", tag=f"acc{i}")
+                    turned_sum(obank, low_t, rise_t, a, b - a)
+                    nc.scalar.copy(res[:, a:b], obank[:, 0 : b - a])
+                    nc.scalar.dma_start(out=out[m * P : (m + 1) * P, a:b], in_=res[:, a:b])
             else:
-                for d in range(3):
-                    nc.vector.tensor_copy(g[d][:], y[m][:].indirect(places[d][:]))
-                nc.vector.tensor_tensor(t[0][:], g[0][:], g[1][:], ALU.max)
-                nc.vector.tensor_tensor(t[1][:], g[0][:], g[1][:], ALU.min)
+                u = keep.tile([P, V], F32, name="u")
                 for a, b in parts:
-                    nc.vector.tensor_tensor(t[2][:, a:b], t[0][:, a:b], g[2][:, a:b], ALU.min)
+                    nc.vector.scalar_tensor_tensor(u[:, a:b], p[:, a:b], 0.0, t[:, a:b], ALU.min, ALU.max)
                 for a, b in parts:
-                    nc.vector.tensor_tensor(res[:, a:b], t[1][:, a:b], t[2][:, a:b], ALU.max)
+                    nc.vector.tensor_tensor(res[:, a:b], u[:, a:b], base[:, a:b], ALU.add)
                     nc.sync.dma_start(out=out[m * P : (m + 1) * P, a:b], in_=res[:, a:b])

@@ -19,12 +19,20 @@ ACT = mybir.ActivationFunctionType
 
 P = 128
 PACK = 4
+LIST_COLUMN = 16
+BANK = 512
+QUADRANT = 32
+SCALE_ROWS = 4
 HALF = S // 2
-PIECES = [256,256,256,128,128]
-SHARE = True
-FUSED = True
-WARM = True
-CHUNKS = [[1024,1024],[1024,1024],[1024,512],[768,0],[256,256]]
+
+LOAD_ORDER = (2, 0, 1, 3)
+EARLY_SHARED, LAST_SHARED = LOAD_ORDER[0], LOAD_ORDER[-1]
+
+LAST_PLANE_CHUNKS = ((1024, 1024), (1024, 1024), (1024, 512), (768, 0), (256, 256))
+
+PIECES = (256, 256, 256, 128, 128)
+
+TARGET_HALVES = ((0, V // 2), (V // 2, V))
 
 
 def tile_picked_median_gelu_e_kernel(
@@ -37,74 +45,68 @@ def tile_picked_median_gelu_e_kernel(
 
         rows = xT.rearrange("(p j) t -> p j t", j=PACK)
         planes = [keep.tile([P, T], F32, name=f"plane{j}") for j in range(PACK)]
-        picks = keep.tile([P, S // 16], U16, name="picks")
-        places = [keep.tile([P, V // 16], U16, name=f"places{d}") for d in range(3)]
+        picks = keep.tile([P, S // LIST_COLUMN], U16, name="picks")
+        places = [keep.tile([P, V // LIST_COLUMN], U16, name=f"places{d}") for d in range(3)]
         w_words = keep.tile([P, 2 * N], U8, name="w_words", align_bytes=64)
         w_scales = keep.tile([P, N], U8, name="w_scales", align_bytes=64)
         grouped = [keep.tile([P, HALF, PACK], BF16, name=f"grouped{h}", align_bytes=64) for h in range(2)]
         codes = keep.tile([P, S], U32, name="codes", align_bytes=64)
         scales = keep.tile([P, S], U8, name="scales", align_bytes=64)
-        y = [keep.tile([P, S], F32, name=f"y{m}") for m in range(2)]
+        y = [keep.tile([P, S], F32, name=f"y{m}") for m in range(N // P)]
 
-        order = [2, 0, 1, 3] if SHARE else [0, 1, 2, 3]
-        if WARM:
-            warm = keep.tile([P, 2], F32, name="warm")
-            nc.vector.memset(warm[:, 0:1], 0.0)
-            nc.scalar.activation(warm[:, 1:2], warm[:, 0:1], ACT.Gelu_apprx_tanh)
+        warm = keep.tile([P, 2], F32, name="warm")
+        nc.vector.memset(warm[:, 0:1], 0.0)
+        nc.scalar.activation(warm[:, 1:2], warm[:, 0:1], ACT.Gelu_apprx_tanh)
 
         nc.gpsimd.memset(w_scales[:].bitcast(I32), 0)
 
         ident = keep.tile([P, P], F32, name="ident")
         make_identity(nc, ident[:])
 
-        def pick(h):
-            return picks[:, h * (HALF // 16) : (h + 1) * (HALF // 16)]
+        rounded = {j: keep.tile([P, T], BF16, name=f"rounded{j}") for j in (EARLY_SHARED, LAST_SHARED)}
 
-        def vgather(j, h):
-            nc.vector.tensor_copy(grouped[h][:, :, j], planes[j][:].indirect(pick(h)))
+        def picks_of(h):
+            return picks[:, h * (HALF // LIST_COLUMN) : (h + 1) * (HALF // LIST_COLUMN)]
 
-        halves = {}
-        if SHARE:
-            for j in (2, 3):
-                halves[j] = keep.tile([P, T], BF16, name=f"rounded{j}")
+        def load_last_plane():
+            j = LAST_SHARED
+            c0 = 0
+            for width, on_scalar in LAST_PLANE_CHUNKS:
+                split, c1 = c0 + on_scalar, c0 + width
+                nc.sync.dma_start(out=planes[j][:, c0:c1], in_=rows[:, j, c0:c1])
+                if split > c0:
+                    nc.scalar.copy(rounded[j][:, c0:split], planes[j][:, c0:split])
+                if split < c1:
+                    nc.vector.tensor_copy(rounded[j][:, split:c1], planes[j][:, split:c1])
+                c0 = c1
 
-        def sgather(j):
-            nc.scalar.activation(grouped[1][:, :, j], halves[j][:].indirect(pick(1)), ACT.Copy)
+        def load_weights_and_places():
+            nc.sync.dma_start(out=w_words[:].bitcast(I32), in_=w1_words[0].bitcast(I32))
+            for r in range(P // QUADRANT):
+                nc.sync.dma_start(
+                    out=w_scales[QUADRANT * r : QUADRANT * r + SCALE_ROWS, :].bitcast(I32),
+                    in_=w1_scales[0, SCALE_ROWS * r : SCALE_ROWS * (r + 1), :].bitcast(I32),
+                )
+            for d, pos in enumerate((pos1, pos2, pos3)):
+                nc.sync.dma_start(places[d][:], pos)
 
-        for i, j in enumerate(order):
-            if SHARE and j == 3:
-                c0 = 0
-                for w, ws in CHUNKS:
-                    nc.sync.dma_start(out=planes[j][:, c0 : c0 + w], in_=rows[:, j, c0 : c0 + w])
-                    if ws > 0:
-                        nc.scalar.copy(halves[j][:, c0 : c0 + ws], planes[j][:, c0 : c0 + ws])
-                    if ws < w:
-                        nc.vector.tensor_copy(halves[j][:, c0 + ws : c0 + w], planes[j][:, c0 + ws : c0 + w])
-                    c0 = c0 + w
+        for j in LOAD_ORDER:
+            if j == LAST_SHARED:
+                load_last_plane()
+                load_weights_and_places()
             else:
                 nc.sync.dma_start(out=planes[j][:], in_=rows[:, j, :])
-            if i == 0:
+            if j == EARLY_SHARED:
                 nc.sync.dma_start(picks[:], offs)
-            if i == 3:
-                nc.sync.dma_start(out=w_words[:].bitcast(I32), in_=w1_words[0].bitcast(I32))
-                for q in range(4):
-                    nc.sync.dma_start(
-                        out=w_scales[32 * q : 32 * q + 4, :].bitcast(I32),
-                        in_=w1_scales[0, 4 * q : 4 * q + 4, :].bitcast(I32),
-                    )
-                for d, src in enumerate((pos1, pos2, pos3)):
-                    nc.sync.dma_start(places[d][:], src)
-            if SHARE and j == 2:
-                nc.scalar.copy(halves[j][:], planes[j][:])
-            vgather(j, 0)
-            if SHARE and j >= 2:
-                sgather(j)
+                nc.scalar.copy(rounded[j][:], planes[j][:])
+            nc.vector.tensor_copy(grouped[0][:, :, j], planes[j][:].indirect(picks_of(0)))
+            if j in rounded:
+                nc.scalar.activation(grouped[1][:, :, j], rounded[j][:].indirect(picks_of(1)), ACT.Copy)
             else:
-                vgather(j, 1)
+                nc.vector.tensor_copy(grouped[1][:, :, j], planes[j][:].indirect(picks_of(1)))
 
-
-        def product(m, c0, width, tag):
-            acc = psum.tile([P, 512], F32, name=tag, tag=tag)
+        def product(m, c0, width, bank_tag):
+            acc = psum.tile([P, BANK], F32, name=bank_tag, tag=bank_tag)
             nc.tensor.matmul_mx(
                 out=acc[:, 0:width],
                 lhsT=w_words[:, 2 * P * m : 2 * P * (m + 1)].bitcast(FP4X4),
@@ -117,67 +119,73 @@ def tile_picked_median_gelu_e_kernel(
             nc.scalar.activation(y[m][:, c0 : c0 + width], acc[:, 0:width], ACT.Gelu_apprx_tanh)
 
         c0 = 0
-        for i, w in enumerate(PIECES):
-            h, r = divmod(c0, HALF)
+        for i, width in enumerate(PIECES):
+            h, s0 = divmod(c0, HALF)
             nc.vector.quantize_mx(
-                out=codes[:, c0 : c0 + w].bitcast(FP8X4),
-                scales=scales[:, c0 : c0 + w],
-                in_=grouped[h][:, r : r + w, :].rearrange("p s j -> p (s j)"),
+                out=codes[:, c0 : c0 + width].bitcast(FP8X4),
+                scales=scales[:, c0 : c0 + width],
+                in_=grouped[h][:, s0 : s0 + width, :].rearrange("p s j -> p (s j)"),
             )
-            product(0, c0, w, f"acc{i}")
-            c0 = c0 + w
+            product(0, c0, width, f"acc{i}")
+            c0 = c0 + width
         for h in range(2):
             product(1, h * HALF, HALF, f"acc{len(PIECES) - 1 - h}")
 
-        def fetch(m, d, a, b):
-            return y[m][:].indirect(places[d][:, a // 16 : b // 16])
+        def fetch(m, d, v0, v1):
+            return y[m][:].indirect(places[d][:, v0 // LIST_COLUMN : v1 // LIST_COLUMN])
 
-        def turned_sum(bank, first, second, c0, width):
-            for c in range(0, width, P):
-                for i, src in enumerate((first, second)):
-                    nc.tensor.matmul(
-                        bank[:, c : c + P], lhsT=src[:, c0 + c : c0 + c + P], rhs=ident[:],
-                        is_transpose=True, start=(i == 0), stop=(i == 1),
-                    )
-
-        parts = [(0, V // 2), (V // 2, V)]
-        for m in range(2):
-            base = keep.tile([P, V], F32, name=f"base{m}")
+        def differences(m):
+            b = keep.tile([P, V], F32, name=f"b{m}")
             p = keep.tile([P, V], F32, name=f"p{m}")
             q = keep.tile([P, V], F32, name=f"q{m}")
             t = keep.tile([P, V], F32, name=f"t{m}")
-            res = keep.tile([P, V], F32, name=f"res{m}")
-            for a, b in (parts if m == 0 else [(0, V)]):
-                nc.vector.tensor_copy(base[:, a:b], fetch(m, 0, a, b))
-            for a, b in (parts if m == 0 else [(0, V)]):
-                nc.vector.tensor_tensor(p[:, a:b], fetch(m, 1, a, b), base[:, a:b], ALU.subtract)
-            for a, b in (parts if m == 0 else [(0, V)]):
-                nc.vector.tensor_tensor(q[:, a:b], fetch(m, 2, a, b), base[:, a:b], ALU.subtract)
-            for a, b in parts:
-                nc.vector.scalar_tensor_tensor(t[:, a:b], p[:, a:b], 0.0, q[:, a:b], ALU.max, ALU.min)
-            if m == 0:
-                nb = keep.tile([P, V], F32, name="nb")
-                n = keep.tile([P, V], F32, name="n")
-                low_t = keep.tile([P, V], F32, name="low_t")
-                rise_t = keep.tile([P, V], F32, name="rise_t")
-                nc.scalar.activation(nb[:], base[:], ACT.Copy, scale=-1.0)
-                nc.scalar.activation(n[:], p[:], ACT.Relu, scale=-1.0)
-                lbank = psum.tile([P, 512], F32, name="lbank", tag="lbank")
-                turned_sum(lbank, nb, n, 0, V)
-                nc.scalar.activation(low_t[:], lbank[:], ACT.Copy, scale=-1.0)
-                for i, (a, b) in enumerate(parts):
-                    ubank = psum.tile([P, 512], F32, name=f"ubank{i}", tag=f"ubank{i}")
-                    turned_sum(ubank, n, t, a, b - a)
-                    nc.scalar.activation(rise_t[:, a:b], ubank[:, 0 : b - a], ACT.Relu)
-                for i, (a, b) in enumerate(parts):
-                    obank = psum.tile([P, 512], F32, name=f"obank{i}", tag=f"acc{i}")
-                    turned_sum(obank, low_t, rise_t, a, b - a)
-                    nc.scalar.copy(res[:, a:b], obank[:, 0 : b - a])
-                    nc.scalar.dma_start(out=out[m * P : (m + 1) * P, a:b], in_=res[:, a:b])
-            else:
-                u = keep.tile([P, V], F32, name="u")
-                for a, b in parts:
-                    nc.vector.scalar_tensor_tensor(u[:, a:b], p[:, a:b], 0.0, t[:, a:b], ALU.min, ALU.max)
-                for a, b in parts:
-                    nc.vector.tensor_tensor(res[:, a:b], u[:, a:b], base[:, a:b], ALU.add)
-                    nc.sync.dma_start(out=out[m * P : (m + 1) * P, a:b], in_=res[:, a:b])
+            median = keep.tile([P, V], F32, name=f"median{m}")
+            for v0, v1 in TARGET_HALVES:
+                nc.vector.tensor_copy(b[:, v0:v1], fetch(m, 0, v0, v1))
+            for v0, v1 in TARGET_HALVES:
+                nc.vector.tensor_tensor(p[:, v0:v1], fetch(m, 1, v0, v1), b[:, v0:v1], ALU.subtract)
+            for v0, v1 in TARGET_HALVES:
+                nc.vector.tensor_tensor(q[:, v0:v1], fetch(m, 2, v0, v1), b[:, v0:v1], ALU.subtract)
+            for v0, v1 in TARGET_HALVES:
+                nc.vector.scalar_tensor_tensor(t[:, v0:v1], p[:, v0:v1], 0.0, q[:, v0:v1], ALU.max, ALU.min)
+            return b, p, t, median
+
+        def turned_sum(bank, first, second, v0, v1):
+            for c in range(v0, v1, P):
+                for i, term in enumerate((first, second)):
+                    nc.tensor.matmul(
+                        bank[:, c - v0 : c - v0 + P],
+                        lhsT=term[:, c : c + P],
+                        rhs=ident[:],
+                        is_transpose=True,
+                        start=(i == 0),
+                        stop=(i == 1),
+                    )
+
+        b, p, t, median = differences(0)
+        minus_b = keep.tile([P, V], F32, name="minus_b")
+        n = keep.tile([P, V], F32, name="n")
+        low_turned = keep.tile([P, V], F32, name="low_turned")
+        rise_turned = keep.tile([P, V], F32, name="rise_turned")
+        nc.scalar.activation(minus_b[:], b[:], ACT.Copy, scale=-1.0)
+        nc.scalar.activation(n[:], p[:], ACT.Relu, scale=-1.0)
+        low_bank = psum.tile([P, BANK], F32, name="low_bank")
+        turned_sum(low_bank, minus_b, n, 0, V)
+        nc.scalar.activation(low_turned[:], low_bank[:], ACT.Copy, scale=-1.0)
+        for i, (v0, v1) in enumerate(TARGET_HALVES):
+            rise_bank = psum.tile([P, BANK], F32, name=f"rise_bank{i}")
+            turned_sum(rise_bank, n, t, v0, v1)
+            nc.scalar.activation(rise_turned[:, v0:v1], rise_bank[:, 0 : v1 - v0], ACT.Relu)
+        for i, (v0, v1) in enumerate(TARGET_HALVES):
+            median_bank = psum.tile([P, BANK], F32, name=f"median_bank{i}", tag=f"acc{i}")
+            turned_sum(median_bank, low_turned, rise_turned, v0, v1)
+            nc.scalar.copy(median[:, v0:v1], median_bank[:, 0 : v1 - v0])
+            nc.scalar.dma_start(out=out[0:P, v0:v1], in_=median[:, v0:v1])
+
+        b, p, t, median = differences(1)
+        clamped = keep.tile([P, V], F32, name="clamped")
+        for v0, v1 in TARGET_HALVES:
+            nc.vector.scalar_tensor_tensor(clamped[:, v0:v1], p[:, v0:v1], 0.0, t[:, v0:v1], ALU.min, ALU.max)
+        for v0, v1 in TARGET_HALVES:
+            nc.vector.tensor_tensor(median[:, v0:v1], clamped[:, v0:v1], b[:, v0:v1], ALU.add)
+            nc.sync.dma_start(out=out[P : 2 * P, v0:v1], in_=median[:, v0:v1])

@@ -25,10 +25,10 @@ QUADRANT = 32
 SCALE_ROWS = 4
 HALF = S // 2
 
-LOAD_ORDER = (2, 0, 1, 3)
-EARLY_SHARED, LAST_SHARED = LOAD_ORDER[0], LOAD_ORDER[-1]
-
-LAST_PLANE_CHUNKS = ((1024, 1024), (1024, 1024), (1024, 512), (768, 0), (256, 256))
+SHARED_CHUNKS = {
+    2: ((2048, 2048), (2048, 640)),
+    3: ((2816, 928), (960, 320), (320, 320)),
+}
 
 PIECES = (256, 256, 256, 128, 128)
 
@@ -63,15 +63,14 @@ def tile_picked_median_gelu_e_kernel(
         ident = keep.tile([P, P], F32, name="ident")
         make_identity(nc, ident[:])
 
-        rounded = {j: keep.tile([P, T], BF16, name=f"rounded{j}") for j in (EARLY_SHARED, LAST_SHARED)}
+        rounded = {j: keep.tile([P, T], BF16, name=f"rounded{j}") for j in SHARED_CHUNKS}
 
         def picks_of(h):
             return picks[:, h * (HALF // LIST_COLUMN) : (h + 1) * (HALF // LIST_COLUMN)]
 
-        def load_last_plane():
-            j = LAST_SHARED
+        def load_shared_plane(j):
             c0 = 0
-            for width, on_scalar in LAST_PLANE_CHUNKS:
+            for width, on_scalar in SHARED_CHUNKS[j]:
                 split, c1 = c0 + on_scalar, c0 + width
                 nc.sync.dma_start(out=planes[j][:, c0:c1], in_=rows[:, j, c0:c1])
                 if split > c0:
@@ -90,15 +89,15 @@ def tile_picked_median_gelu_e_kernel(
             for d, pos in enumerate((pos1, pos2, pos3)):
                 nc.sync.dma_start(places[d][:], pos)
 
-        for j in LOAD_ORDER:
-            if j == LAST_SHARED:
-                load_last_plane()
-                load_weights_and_places()
+        for j in range(PACK):
+            if j in SHARED_CHUNKS:
+                load_shared_plane(j)
             else:
                 nc.sync.dma_start(out=planes[j][:], in_=rows[:, j, :])
-            if j == EARLY_SHARED:
+            if j == 0:
                 nc.sync.dma_start(picks[:], offs)
-                nc.scalar.copy(rounded[j][:], planes[j][:])
+            if j == PACK - 1:
+                load_weights_and_places()
             nc.vector.tensor_copy(grouped[0][:, :, j], planes[j][:].indirect(picks_of(0)))
             if j in rounded:
                 nc.scalar.activation(grouped[1][:, :, j], rounded[j][:].indirect(picks_of(1)), ACT.Copy)

@@ -30,7 +30,7 @@ SHARED_CHUNKS = {
     3: ((2816, 928), (960, 320), (320, 320)),
 }
 
-PIECES = (256, 256, 256, 128, 128)
+PIECES = (256, 256, 128, 128, 128, 128)
 
 TARGET_HALVES = ((0, V // 2), (V // 2, V))
 
@@ -141,10 +141,13 @@ def tile_picked_median_gelu_e_kernel(
             median = keep.tile([P, V], F32, name=f"median{m}")
             for v0, v1 in TARGET_HALVES:
                 nc.vector.tensor_copy(b[:, v0:v1], fetch(m, 0, v0, v1))
-            for v0, v1 in TARGET_HALVES:
+            for i, (v0, v1) in enumerate(TARGET_HALVES):
                 nc.vector.tensor_tensor(p[:, v0:v1], fetch(m, 1, v0, v1), b[:, v0:v1], ALU.subtract)
-            for v0, v1 in TARGET_HALVES:
-                nc.vector.tensor_tensor(q[:, v0:v1], fetch(m, 2, v0, v1), b[:, v0:v1], ALU.subtract)
+                if i == 0 and m == 1:
+                    nc.vector.tensor_tensor(q[:], fetch(m, 2, 0, V), b[:], ALU.subtract)
+            if m == 0:
+                for v0, v1 in TARGET_HALVES:
+                    nc.vector.tensor_tensor(q[:, v0:v1], fetch(m, 2, v0, v1), b[:, v0:v1], ALU.subtract)
             for v0, v1 in TARGET_HALVES:
                 nc.vector.scalar_tensor_tensor(t[:, v0:v1], p[:, v0:v1], 0.0, q[:, v0:v1], ALU.max, ALU.min)
             return b, p, t, median
@@ -168,7 +171,7 @@ def tile_picked_median_gelu_e_kernel(
         rise_turned = keep.tile([P, V], F32, name="rise_turned")
         nc.scalar.activation(minus_b[:], b[:], ACT.Copy, scale=-1.0)
         nc.scalar.activation(n[:], p[:], ACT.Relu, scale=-1.0)
-        low_bank = psum.tile([P, BANK], F32, name="low_bank")
+        low_bank = psum.tile([P, BANK], F32, name="low_bank", tag="acc2")
         turned_sum(low_bank, minus_b, n, 0, V)
         nc.scalar.activation(low_turned[:], low_bank[:], ACT.Copy, scale=-1.0)
         for i, (v0, v1) in enumerate(TARGET_HALVES):

@@ -133,59 +133,75 @@ def tile_picked_median_gelu_e_kernel(
         def fetch(m, d, v0, v1):
             return y[m][:].indirect(places[d][:, v0 // LIST_COLUMN : v1 // LIST_COLUMN])
 
-        def differences(m):
-            b = keep.tile([P, V], F32, name=f"b{m}")
-            p = keep.tile([P, V], F32, name=f"p{m}")
-            q = keep.tile([P, V], F32, name=f"q{m}")
-            t = keep.tile([P, V], F32, name=f"t{m}")
-            median = keep.tile([P, V], F32, name=f"median{m}")
-            for v0, v1 in TARGET_HALVES:
-                nc.vector.tensor_copy(b[:, v0:v1], fetch(m, 0, v0, v1))
-            for i, (v0, v1) in enumerate(TARGET_HALVES):
-                nc.vector.tensor_tensor(p[:, v0:v1], fetch(m, 1, v0, v1), b[:, v0:v1], ALU.subtract)
-                if i == 0 and m == 1:
-                    nc.vector.tensor_tensor(q[:], fetch(m, 2, 0, V), b[:], ALU.subtract)
-            if m == 0:
-                for v0, v1 in TARGET_HALVES:
-                    nc.vector.tensor_tensor(q[:, v0:v1], fetch(m, 2, v0, v1), b[:, v0:v1], ALU.subtract)
-            for v0, v1 in TARGET_HALVES:
-                nc.vector.scalar_tensor_tensor(t[:, v0:v1], p[:, v0:v1], 0.0, q[:, v0:v1], ALU.max, ALU.min)
-            return b, p, t, median
+        def turned(bank, column, term, c, start, stop):
+            nc.tensor.matmul(
+                bank[:, column : column + P],
+                lhsT=term[:, c : c + P],
+                rhs=ident[:],
+                is_transpose=True,
+                start=start,
+                stop=stop,
+            )
 
-        def turned_sum(bank, first, second, v0, v1):
-            for c in range(v0, v1, P):
-                for i, term in enumerate((first, second)):
-                    nc.tensor.matmul(
-                        bank[:, c - v0 : c - v0 + P],
-                        lhsT=term[:, c : c + P],
-                        rhs=ident[:],
-                        is_transpose=True,
-                        start=(i == 0),
-                        stop=(i == 1),
-                    )
+        def tile_of(name):
+            return keep.tile([P, V], F32, name=name)
 
-        b, p, t, median = differences(0)
-        minus_b = keep.tile([P, V], F32, name="minus_b")
-        n = keep.tile([P, V], F32, name="n")
-        low_turned = keep.tile([P, V], F32, name="low_turned")
-        rise_turned = keep.tile([P, V], F32, name="rise_turned")
-        nc.scalar.activation(minus_b[:], b[:], ACT.Copy, scale=-1.0)
-        nc.scalar.activation(n[:], p[:], ACT.Relu, scale=-1.0)
+        minus_one = keep.tile([P, V // 2], F32, name="minus_one")
+        nc.vector.memset(minus_one[:], -1.0)
+        minus_b, p, q = tile_of("minus_b"), tile_of("p0"), tile_of("q0")
+        n, r, minus_r = tile_of("n"), tile_of("r"), tile_of("minus_r")
+        low_turned, rise_turned = tile_of("low_turned"), tile_of("rise_turned")
+        over_turned, minus_over_turned = tile_of("over_turned"), tile_of("minus_over_turned")
+        median = tile_of("median0")
+        for v0, v1 in TARGET_HALVES:
+            nc.vector.tensor_tensor(minus_b[:, v0:v1], fetch(0, 0, v0, v1), minus_one[:], ALU.mult)
+        for v0, v1 in TARGET_HALVES:
+            nc.vector.tensor_tensor(p[:, v0:v1], fetch(0, 1, v0, v1), minus_b[:, v0:v1], ALU.add)
+        for v0, v1 in TARGET_HALVES:
+            nc.vector.tensor_tensor(q[:, v0:v1], fetch(0, 2, v0, v1), minus_b[:, v0:v1], ALU.add)
+
         low_bank = psum.tile([P, BANK], F32, name="low_bank", tag="acc2")
-        turned_sum(low_bank, minus_b, n, 0, V)
+        for c in range(0, V, P):
+            turned(low_bank, c, minus_b, c, c == 0, False)
+        side_banks = [psum.tile([P, BANK], F32, name=f"side_bank{i}") for i in range(2)]
+        for i, (v0, v1) in enumerate(TARGET_HALVES):
+            width = v1 - v0
+            nc.scalar.activation(n[:, v0:v1], p[:, v0:v1], ACT.Relu, scale=-1.0)
+            nc.scalar.activation(r[:, v0:v1], p[:, v0:v1], ACT.Relu)
+            for c in range(v0, v1, P):
+                turned(low_bank, c, n, c, False, c == V - P)
+            for c in range(v0, v1, P):
+                turned(side_banks[i], c - v0, n, c, c == v0, False)
+            nc.scalar.activation(minus_r[:, v0:v1], r[:, v0:v1], ACT.Copy, scale=-1.0)
+            for c in range(v0, v1, P):
+                turned(side_banks[i], width + c - v0, minus_r, c, False, False)
         nc.scalar.activation(low_turned[:], low_bank[:], ACT.Copy, scale=-1.0)
         for i, (v0, v1) in enumerate(TARGET_HALVES):
-            rise_bank = psum.tile([P, BANK], F32, name=f"rise_bank{i}")
-            turned_sum(rise_bank, n, t, v0, v1)
-            nc.scalar.activation(rise_turned[:, v0:v1], rise_bank[:, 0 : v1 - v0], ACT.Relu)
+            width = v1 - v0
+            for c in range(v0, v1, P):
+                turned(side_banks[i], c - v0, q, c, False, False)
+                turned(side_banks[i], width + c - v0, q, c, False, c == v1 - P)
+            nc.scalar.activation(over_turned[:, v0:v1], side_banks[i][:, width : 2 * width], ACT.Relu)
+            nc.scalar.activation(rise_turned[:, v0:v1], side_banks[i][:, 0:width], ACT.Relu)
+            nc.scalar.activation(minus_over_turned[:, v0:v1], over_turned[:, v0:v1], ACT.Copy, scale=-1.0)
         for i, (v0, v1) in enumerate(TARGET_HALVES):
             median_bank = psum.tile([P, BANK], F32, name=f"median_bank{i}", tag=f"acc{i}")
-            turned_sum(median_bank, low_turned, rise_turned, v0, v1)
+            for k, term in enumerate((low_turned, rise_turned, minus_over_turned)):
+                for c in range(v0, v1, P):
+                    turned(median_bank, c - v0, term, c, k == 0 and c == v0, k == 2 and c == v1 - P)
             nc.scalar.copy(median[:, v0:v1], median_bank[:, 0 : v1 - v0])
             nc.scalar.dma_start(out=out[0:P, v0:v1], in_=median[:, v0:v1])
 
-        b, p, t, median = differences(1)
-        clamped = keep.tile([P, V], F32, name="clamped")
+        b, p, q, t = tile_of("b1"), tile_of("p1"), tile_of("q1"), tile_of("t1")
+        clamped, median = tile_of("clamped"), tile_of("median1")
+        for v0, v1 in TARGET_HALVES:
+            nc.vector.tensor_copy(b[:, v0:v1], fetch(1, 0, v0, v1))
+        for i, (v0, v1) in enumerate(TARGET_HALVES):
+            nc.vector.tensor_tensor(p[:, v0:v1], fetch(1, 1, v0, v1), b[:, v0:v1], ALU.subtract)
+            if i == 0:
+                nc.vector.tensor_tensor(q[:], fetch(1, 2, 0, V), b[:], ALU.subtract)
+        for v0, v1 in TARGET_HALVES:
+            nc.vector.scalar_tensor_tensor(t[:, v0:v1], p[:, v0:v1], 0.0, q[:, v0:v1], ALU.max, ALU.min)
         for v0, v1 in TARGET_HALVES:
             nc.vector.scalar_tensor_tensor(clamped[:, v0:v1], p[:, v0:v1], 0.0, t[:, v0:v1], ALU.min, ALU.max)
         for v0, v1 in TARGET_HALVES:

@@ -25,12 +25,17 @@ QUADRANT = 32
 SCALE_ROWS = 4
 HALF = S // 2
 
-SHARED_CHUNKS = {
-    2: ((2048, 2048), (2048, 640)),
-    3: ((2816, 928), (960, 320), (320, 320)),
-}
+LOADS = (
+    (0, T, 0),
+    (T, T + 1024, 1024),
+    (2 * T + 1024, 3072, 1024),
+    (3 * T, 2816, 960),
+    (3 * T + 2816, 960, 384),
+    (3 * T + 3776, 320, 320),
+)
+SHARED = 2
 
-PIECES = (256, 256, 128, 128, 128, 128)
+PIECES = (128,) * 8
 
 TARGET_HALVES = ((0, V // 2), (V // 2, V))
 
@@ -43,8 +48,8 @@ def tile_picked_median_gelu_e_kernel(
         keep = ctx.enter_context(tc.tile_pool(name="keep", bufs=1))
         psum = ctx.enter_context(tc.psum_pool(name="psum", bufs=1))
 
-        rows = xT.rearrange("(p j) t -> p j t", j=PACK)
-        planes = [keep.tile([P, T], F32, name=f"plane{j}") for j in range(PACK)]
+        rows = xT.rearrange("(p j) t -> p (j t)", j=PACK)
+        flat = keep.tile([P, PACK * T], F32, name="flat")
         picks = keep.tile([P, S // LIST_COLUMN], U16, name="picks")
         places = [keep.tile([P, V // LIST_COLUMN], U16, name=f"places{d}") for d in range(3)]
         w_words = keep.tile([P, 2 * N], U8, name="w_words", align_bytes=64)
@@ -63,21 +68,10 @@ def tile_picked_median_gelu_e_kernel(
         ident = keep.tile([P, P], F32, name="ident")
         make_identity(nc, ident[:])
 
-        rounded = {j: keep.tile([P, T], BF16, name=f"rounded{j}") for j in SHARED_CHUNKS}
+        rounded = {j: keep.tile([P, T], BF16, name=f"rounded{j}") for j in range(SHARED, PACK)}
 
         def picks_of(h):
             return picks[:, h * (HALF // LIST_COLUMN) : (h + 1) * (HALF // LIST_COLUMN)]
-
-        def load_shared_plane(j):
-            c0 = 0
-            for width, on_scalar in SHARED_CHUNKS[j]:
-                split, c1 = c0 + on_scalar, c0 + width
-                nc.sync.dma_start(out=planes[j][:, c0:c1], in_=rows[:, j, c0:c1])
-                if split > c0:
-                    nc.scalar.copy(rounded[j][:, c0:split], planes[j][:, c0:split])
-                if split < c1:
-                    nc.vector.tensor_copy(rounded[j][:, split:c1], planes[j][:, split:c1])
-                c0 = c1
 
         def load_weights_and_places():
             nc.sync.dma_start(out=w_words[:].bitcast(I32), in_=w1_words[0].bitcast(I32))
@@ -89,20 +83,27 @@ def tile_picked_median_gelu_e_kernel(
             for d, pos in enumerate((pos1, pos2, pos3)):
                 nc.sync.dma_start(places[d][:], pos)
 
-        for j in range(PACK):
-            if j in SHARED_CHUNKS:
-                load_shared_plane(j)
-            else:
-                nc.sync.dma_start(out=planes[j][:], in_=rows[:, j, :])
-            if j == 0:
+        for c0, width, on_scalar in LOADS:
+            c1 = c0 + width
+            nc.sync.dma_start(out=flat[:, c0:c1], in_=rows[:, c0:c1])
+            if c0 == 0:
                 nc.sync.dma_start(picks[:], offs)
-            if j == PACK - 1:
+            if c1 == PACK * T:
                 load_weights_and_places()
-            nc.vector.tensor_copy(grouped[0][:, :, j], planes[j][:].indirect(picks_of(0)))
-            if j in rounded:
-                nc.scalar.activation(grouped[1][:, :, j], rounded[j][:].indirect(picks_of(1)), ACT.Copy)
-            else:
-                nc.vector.tensor_copy(grouped[1][:, :, j], planes[j][:].indirect(picks_of(1)))
+            first = max(c0, SHARED * T)
+            if first < c1:
+                j, t0 = divmod(first, T)
+                split, t1 = t0 + on_scalar, c1 - j * T
+                nc.scalar.copy(rounded[j][:, t0:split], flat[:, first : first + on_scalar])
+                if split < t1:
+                    nc.vector.tensor_copy(rounded[j][:, split:t1], flat[:, first + on_scalar : c1])
+            for j in range(c0 // T, c1 // T):
+                plane = flat[:, j * T : (j + 1) * T]
+                nc.vector.tensor_copy(grouped[0][:, :, j], plane.indirect(picks_of(0)))
+                if j in rounded:
+                    nc.scalar.activation(grouped[1][:, :, j], rounded[j][:].indirect(picks_of(1)), ACT.Copy)
+                else:
+                    nc.vector.tensor_copy(grouped[1][:, :, j], plane.indirect(picks_of(1)))
 
         def product(m, c0, width, bank_tag):
             acc = psum.tile([P, BANK], F32, name=bank_tag, tag=bank_tag)
@@ -163,7 +164,7 @@ def tile_picked_median_gelu_e_kernel(
         low_bank = psum.tile([P, BANK], F32, name="low_bank", tag="acc2")
         for c in range(0, V, P):
             turned(low_bank, c, minus_b, c, c == 0, False)
-        side_banks = [psum.tile([P, BANK], F32, name=f"side_bank{i}") for i in range(2)]
+        side_banks = [psum.tile([P, BANK], F32, name=f"side_bank{i}", tag=f"acc{3 + i}") for i in range(2)]
         for i, (v0, v1) in enumerate(TARGET_HALVES):
             width = v1 - v0
             nc.scalar.activation(n[:, v0:v1], p[:, v0:v1], ACT.Relu, scale=-1.0)

@@ -158,8 +158,7 @@ def tile_picked_median_gelu_e_kernel(
             nc.vector.tensor_tensor(minus_b[:, v0:v1], fetch(0, 0, v0, v1), minus_one[:], ALU.mult)
         for v0, v1 in TARGET_HALVES:
             nc.vector.tensor_tensor(p[:, v0:v1], fetch(0, 1, v0, v1), minus_b[:, v0:v1], ALU.add)
-        for v0, v1 in TARGET_HALVES:
-            nc.vector.tensor_tensor(q[:, v0:v1], fetch(0, 2, v0, v1), minus_b[:, v0:v1], ALU.add)
+        nc.vector.tensor_tensor(q[:], fetch(0, 2, 0, V), minus_b[:], ALU.add)
 
         low_bank = psum.tile([P, BANK], F32, name="low_bank", tag="acc2")
         for c in range(0, V, P):

@@ -1,7 +1,6 @@
 from contextlib import ExitStack
 
 import concourse.mybir as mybir
-from concourse.masks import make_identity
 
 K, T, S, V, N = 512, 4096, 1024, 512, 256
 FLOPS = 2 * K * N * S
@@ -64,9 +63,6 @@ def tile_picked_median_gelu_e_kernel(
         nc.scalar.activation(warm[:, 1:2], warm[:, 0:1], ACT.Gelu_apprx_tanh)
 
         nc.gpsimd.memset(w_scales[:].bitcast(I32), 0)
-
-        ident = keep.tile([P, P], F32, name="ident")
-        make_identity(nc, ident[:])
 
         rounded = {j: keep.tile([P, T], BF16, name=f"rounded{j}") for j in range(SHARED, PACK)}
 
@@ -134,76 +130,55 @@ def tile_picked_median_gelu_e_kernel(
         def fetch(m, d, v0, v1):
             return y[m][:].indirect(places[d][:, v0 // LIST_COLUMN : v1 // LIST_COLUMN])
 
-        def turned(bank, column, term, c, start, stop):
-            nc.tensor.matmul(
-                bank[:, column : column + P],
-                lhsT=term[:, c : c + P],
-                rhs=ident[:],
-                is_transpose=True,
-                start=start,
-                stop=stop,
-            )
+        def on_vector(dst, m, d, v0, v1):
+            nc.vector.tensor_copy(dst[:, v0:v1], fetch(m, d, v0, v1))
 
-        def tile_of(name):
-            return keep.tile([P, V], F32, name=name)
+        def on_scalar_engine(dst, m, d, v0, v1):
+            nc.scalar.activation(dst[:, v0:v1], fetch(m, d, v0, v1), ACT.Copy)
 
-        minus_one = keep.tile([P, V // 2], F32, name="minus_one")
-        nc.vector.memset(minus_one[:], -1.0)
-        minus_b, p, q = tile_of("minus_b"), tile_of("p0"), tile_of("q0")
-        n, r, minus_r = tile_of("n"), tile_of("r"), tile_of("minus_r")
-        low_turned, rise_turned = tile_of("low_turned"), tile_of("rise_turned")
-        over_turned, minus_over_turned = tile_of("over_turned"), tile_of("minus_over_turned")
-        median = tile_of("median0")
-        for v0, v1 in TARGET_HALVES:
-            nc.vector.tensor_tensor(minus_b[:, v0:v1], fetch(0, 0, v0, v1), minus_one[:], ALU.mult)
-        for v0, v1 in TARGET_HALVES:
-            nc.vector.tensor_tensor(p[:, v0:v1], fetch(0, 1, v0, v1), minus_b[:, v0:v1], ALU.add)
-        nc.vector.tensor_tensor(q[:], fetch(0, 2, 0, V), minus_b[:], ALU.add)
+        def tiles_of(name):
+            return [keep.tile([P, V], F32, name=f"{name}{m}") for m in range(N // P)]
 
-        low_bank = psum.tile([P, BANK], F32, name="low_bank", tag="acc2")
-        for c in range(0, V, P):
-            turned(low_bank, c, minus_b, c, c == 0, False)
-        side_banks = [psum.tile([P, BANK], F32, name=f"side_bank{i}", tag=f"acc{3 + i}") for i in range(2)]
-        for i, (v0, v1) in enumerate(TARGET_HALVES):
-            width = v1 - v0
-            nc.scalar.activation(n[:, v0:v1], p[:, v0:v1], ACT.Relu, scale=-1.0)
-            nc.scalar.activation(r[:, v0:v1], p[:, v0:v1], ACT.Relu)
-            for c in range(v0, v1, P):
-                turned(low_bank, c, n, c, False, c == V - P)
-            for c in range(v0, v1, P):
-                turned(side_banks[i], c - v0, n, c, c == v0, False)
-            nc.scalar.activation(minus_r[:, v0:v1], r[:, v0:v1], ACT.Copy, scale=-1.0)
-            for c in range(v0, v1, P):
-                turned(side_banks[i], width + c - v0, minus_r, c, False, False)
-        nc.scalar.activation(low_turned[:], low_bank[:], ACT.Copy, scale=-1.0)
-        for i, (v0, v1) in enumerate(TARGET_HALVES):
-            width = v1 - v0
-            for c in range(v0, v1, P):
-                turned(side_banks[i], c - v0, q, c, False, False)
-                turned(side_banks[i], width + c - v0, q, c, False, c == v1 - P)
-            nc.scalar.activation(over_turned[:, v0:v1], side_banks[i][:, width : 2 * width], ACT.Relu)
-            nc.scalar.activation(rise_turned[:, v0:v1], side_banks[i][:, 0:width], ACT.Relu)
-            nc.scalar.activation(minus_over_turned[:, v0:v1], over_turned[:, v0:v1], ACT.Copy, scale=-1.0)
-        for i, (v0, v1) in enumerate(TARGET_HALVES):
-            median_bank = psum.tile([P, BANK], F32, name=f"median_bank{i}", tag=f"acc{i}")
-            for k, term in enumerate((low_turned, rise_turned, minus_over_turned)):
-                for c in range(v0, v1, P):
-                    turned(median_bank, c - v0, term, c, k == 0 and c == v0, k == 2 and c == v1 - P)
-            nc.scalar.copy(median[:, v0:v1], median_bank[:, 0 : v1 - v0])
-            nc.scalar.dma_start(out=out[0:P, v0:v1], in_=median[:, v0:v1])
+        a, b, c = tiles_of("a"), tiles_of("b"), tiles_of("c")
+        low, high, capped, median = tiles_of("low"), tiles_of("high"), tiles_of("capped"), tiles_of("median")
 
-        b, p, q, t = tile_of("b1"), tile_of("p1"), tile_of("q1"), tile_of("t1")
-        clamped, median = tile_of("clamped"), tile_of("median1")
-        for v0, v1 in TARGET_HALVES:
-            nc.vector.tensor_copy(b[:, v0:v1], fetch(1, 0, v0, v1))
-        for i, (v0, v1) in enumerate(TARGET_HALVES):
-            nc.vector.tensor_tensor(p[:, v0:v1], fetch(1, 1, v0, v1), b[:, v0:v1], ALU.subtract)
-            if i == 0:
-                nc.vector.tensor_tensor(q[:], fetch(1, 2, 0, V), b[:], ALU.subtract)
-        for v0, v1 in TARGET_HALVES:
-            nc.vector.scalar_tensor_tensor(t[:, v0:v1], p[:, v0:v1], 0.0, q[:, v0:v1], ALU.max, ALU.min)
-        for v0, v1 in TARGET_HALVES:
-            nc.vector.scalar_tensor_tensor(clamped[:, v0:v1], p[:, v0:v1], 0.0, t[:, v0:v1], ALU.min, ALU.max)
-        for v0, v1 in TARGET_HALVES:
-            nc.vector.tensor_tensor(median[:, v0:v1], clamped[:, v0:v1], b[:, v0:v1], ALU.add)
-            nc.sync.dma_start(out=out[P : 2 * P, v0:v1], in_=median[:, v0:v1])
+        def bounds(m, v0, v1):
+            nc.vector.tensor_tensor(high[m][:, v0:v1], a[m][:, v0:v1], b[m][:, v0:v1], ALU.max)
+            nc.vector.tensor_tensor(low[m][:, v0:v1], a[m][:, v0:v1], b[m][:, v0:v1], ALU.min)
+
+        def cap(m, v0, v1):
+            nc.vector.tensor_tensor(capped[m][:, v0:v1], high[m][:, v0:v1], c[m][:, v0:v1], ALU.min)
+
+        def finish(m, v0, v1):
+            nc.vector.tensor_tensor(median[m][:, v0:v1], low[m][:, v0:v1], capped[m][:, v0:v1], ALU.max)
+
+        def store(m, v0, v1):
+            nc.sync.dma_start(out=out[m * P : (m + 1) * P, v0:v1], in_=median[m][:, v0:v1])
+
+        mid = V // 2
+        on_vector(a[0], 0, 0, 0, V)
+        on_vector(b[0], 0, 1, 0, mid)
+        on_scalar_engine(b[0], 0, 1, mid, V)
+        on_scalar_engine(c[0], 0, 2, 0, V)
+        bounds(0, mid, V)
+        bounds(0, 0, mid)
+        cap(0, 0, V)
+        for d, dst in enumerate((a, b, c)):
+            on_scalar_engine(dst[1], 1, d, 0, mid)
+        on_vector(a[1], 1, 0, mid, V)
+        finish(0, 0, V)
+        store(0, 0, V)
+        last = V - V // 4
+        on_scalar_engine(b[1], 1, 1, mid, V)
+        on_scalar_engine(c[1], 1, 2, mid, last)
+        on_scalar_engine(c[1], 1, 2, last, V)
+        bounds(1, 0, mid)
+        cap(1, 0, mid)
+        bounds(1, mid, V)
+        finish(1, 0, mid)
+        store(1, 0, mid)
+        cap(1, mid, last)
+        cap(1, last, V)
+        finish(1, mid, last)
+        finish(1, last, V)
+        store(1, mid, V)

@@ -24,17 +24,12 @@ QUADRANT = 32
 SCALE_ROWS = 4
 HALF = S // 2
 
-LOADS = (
-    (0, T, 0),
-    (T, T + 1024, 1024),
-    (2 * T + 1024, 3072, 1024),
-    (3 * T, 2816, 960),
-    (3 * T + 2816, 960, 384),
-    (3 * T + 3776, 320, 320),
-)
+LOADS = ((0, 2), (2, 3), (3, 4))
 SHARED = 2
+LAID_BY_VECTOR = 128
 
-PIECES = (128,) * 8
+PIECE = 128
+GELU_GROUPS = (256, 256, 256, 128, 128)
 
 TARGET_HALVES = ((0, V // 2), (V // 2, V))
 
@@ -62,12 +57,10 @@ def tile_picked_median_gelu_e_kernel(
         nc.vector.memset(warm[:, 0:1], 0.0)
         nc.scalar.activation(warm[:, 1:2], warm[:, 0:1], ACT.Gelu_apprx_tanh)
 
-        nc.gpsimd.memset(w_scales[:].bitcast(I32), 0)
+        nc.vector.memset(w_scales[:].bitcast(I32), 0)
 
-        rounded = {j: keep.tile([P, T], BF16, name=f"rounded{j}") for j in range(SHARED, PACK)}
-
-        def picks_of(h):
-            return picks[:, h * (HALF // LIST_COLUMN) : (h + 1) * (HALF // LIST_COLUMN)]
+        def picks_of(s0, s1):
+            return picks[:, s0 // LIST_COLUMN : s1 // LIST_COLUMN]
 
         def load_weights_and_places():
             nc.sync.dma_start(out=w_words[:].bitcast(I32), in_=w1_words[0].bitcast(I32))
@@ -79,32 +72,31 @@ def tile_picked_median_gelu_e_kernel(
             for d, pos in enumerate((pos1, pos2, pos3)):
                 nc.sync.dma_start(places[d][:], pos)
 
-        for c0, width, on_scalar in LOADS:
-            c1 = c0 + width
-            nc.sync.dma_start(out=flat[:, c0:c1], in_=rows[:, c0:c1])
-            if c0 == 0:
+        quarter = HALF // 2
+        for j0, j1 in LOADS:
+            nc.sync.dma_start(out=flat[:, j0 * T : j1 * T], in_=rows[:, j0 * T : j1 * T])
+            if j0 == 0:
                 nc.sync.dma_start(picks[:], offs)
-            if c1 == PACK * T:
+            if j1 == PACK:
                 load_weights_and_places()
-            first = max(c0, SHARED * T)
-            if first < c1:
-                j, t0 = divmod(first, T)
-                split, t1 = t0 + on_scalar, c1 - j * T
-                nc.scalar.copy(rounded[j][:, t0:split], flat[:, first : first + on_scalar])
-                if split < t1:
-                    nc.vector.tensor_copy(rounded[j][:, split:t1], flat[:, first + on_scalar : c1])
-            for j in range(c0 // T, c1 // T):
+            for j in range(j0, j1):
                 plane = flat[:, j * T : (j + 1) * T]
-                nc.vector.tensor_copy(grouped[0][:, :, j], plane.indirect(picks_of(0)))
-                if j in rounded:
-                    nc.scalar.activation(grouped[1][:, :, j], rounded[j][:].indirect(picks_of(1)), ACT.Copy)
-                else:
-                    nc.vector.tensor_copy(grouped[1][:, :, j], plane.indirect(picks_of(1)))
+                nc.vector.tensor_copy(grouped[0][:, :, j], plane.indirect(picks_of(0, HALF)))
+                if j < SHARED:
+                    nc.vector.tensor_copy(grouped[1][:, :, j], plane.indirect(picks_of(HALF, S)))
+                    continue
+                picked = keep.tile([P, HALF], F32, name=f"picked{j}")
+                for s0 in (0, quarter):
+                    nc.scalar.activation(
+                        picked[:, s0 : s0 + quarter], plane.indirect(picks_of(HALF + s0, HALF + s0 + quarter)), ACT.Copy
+                    )
+                nc.vector.tensor_copy(grouped[1][:, 0:LAID_BY_VECTOR, j], picked[:, 0:LAID_BY_VECTOR])
+                for s0, s1 in ((LAID_BY_VECTOR, quarter), (quarter, HALF)):
+                    nc.scalar.copy(grouped[1][:, s0:s1, j], picked[:, s0:s1])
 
-        def product(m, c0, width, bank_tag):
-            acc = psum.tile([P, BANK], F32, name=bank_tag, tag=bank_tag)
+        def product(m, c0, width, acc):
             nc.tensor.matmul_mx(
-                out=acc[:, 0:width],
+                out=acc,
                 lhsT=w_words[:, 2 * P * m : 2 * P * (m + 1)].bitcast(FP4X4),
                 lhsT_scale=w_scales[:, P * m : P * (m + 1)],
                 rhs=codes[:, c0 : c0 + width].bitcast(FP8X4),
@@ -112,20 +104,27 @@ def tile_picked_median_gelu_e_kernel(
                 start=True,
                 stop=True,
             )
-            nc.scalar.activation(y[m][:, c0 : c0 + width], acc[:, 0:width], ACT.Gelu_apprx_tanh)
 
-        c0 = 0
-        for i, width in enumerate(PIECES):
-            h, s0 = divmod(c0, HALF)
-            nc.vector.quantize_mx(
-                out=codes[:, c0 : c0 + width].bitcast(FP8X4),
-                scales=scales[:, c0 : c0 + width],
-                in_=grouped[h][:, s0 : s0 + width, :].rearrange("p s j -> p (s j)"),
-            )
-            product(0, c0, width, f"acc{i}")
-            c0 = c0 + width
+        def bank(tag):
+            return psum.tile([P, BANK], F32, name=tag, tag=tag)
+
+        g0 = 0
+        for i, width in enumerate(GELU_GROUPS):
+            acc = bank(f"acc{i}")
+            for c0 in range(g0, g0 + width, PIECE):
+                h, s0 = divmod(c0, HALF)
+                nc.vector.quantize_mx(
+                    out=codes[:, c0 : c0 + PIECE].bitcast(FP8X4),
+                    scales=scales[:, c0 : c0 + PIECE],
+                    in_=grouped[h][:, s0 : s0 + PIECE, :].rearrange("p s j -> p (s j)"),
+                )
+                product(0, c0, PIECE, acc[:, c0 - g0 : c0 - g0 + PIECE])
+            nc.scalar.activation(y[0][:, g0 : g0 + width], acc[:, 0:width], ACT.Gelu_apprx_tanh)
+            g0 = g0 + width
         for h in range(2):
-            product(1, h * HALF, HALF, f"acc{len(PIECES) - 1 - h}")
+            acc = bank(f"acc{len(GELU_GROUPS) - 1 - h}")
+            product(1, h * HALF, HALF, acc[:])
+            nc.scalar.activation(y[1][:, h * HALF : (h + 1) * HALF], acc[:], ACT.Gelu_apprx_tanh)
 
         def fetch(m, d, v0, v1):
             return y[m][:].indirect(places[d][:, v0 // LIST_COLUMN : v1 // LIST_COLUMN])
@@ -155,30 +154,22 @@ def tile_picked_median_gelu_e_kernel(
         def store(m, v0, v1):
             nc.sync.dma_start(out=out[m * P : (m + 1) * P, v0:v1], in_=median[m][:, v0:v1])
 
-        mid = V // 2
         on_vector(a[0], 0, 0, 0, V)
-        on_vector(b[0], 0, 1, 0, mid)
-        on_scalar_engine(b[0], 0, 1, mid, V)
-        on_scalar_engine(c[0], 0, 2, 0, V)
-        bounds(0, mid, V)
-        bounds(0, 0, mid)
+        on_scalar_engine(b[0], 0, 1, 0, V)
+        on_vector(c[0], 0, 2, 0, V)
+        bounds(0, 0, V)
         cap(0, 0, V)
-        for d, dst in enumerate((a, b, c)):
-            on_scalar_engine(dst[1], 1, d, 0, mid)
-        on_vector(a[1], 1, 0, mid, V)
+        for v0, v1 in TARGET_HALVES:
+            on_scalar_engine(a[1], 1, 0, v0, v1)
+            on_scalar_engine(b[1], 1, 1, v0, v1)
+        for v0, v1 in TARGET_HALVES:
+            on_scalar_engine(c[1], 1, 2, v0, v1)
+        bounds(1, *TARGET_HALVES[0])
         finish(0, 0, V)
         store(0, 0, V)
-        last = V - V // 4
-        on_scalar_engine(b[1], 1, 1, mid, V)
-        on_scalar_engine(c[1], 1, 2, mid, last)
-        on_scalar_engine(c[1], 1, 2, last, V)
-        bounds(1, 0, mid)
-        cap(1, 0, mid)
-        bounds(1, mid, V)
-        finish(1, 0, mid)
-        store(1, 0, mid)
-        cap(1, mid, last)
-        cap(1, last, V)
-        finish(1, mid, last)
-        finish(1, last, V)
-        store(1, mid, V)
+        bounds(1, *TARGET_HALVES[1])
+        for v0, v1 in TARGET_HALVES:
+            cap(1, v0, v1)
+        for v0, v1 in TARGET_HALVES:
+            finish(1, v0, v1)
+            store(1, v0, v1)

@@ -26,12 +26,13 @@ HALF = S // 2
 
 LOADS = ((0, 2), (2, 3), (3, 4))
 SHARED = 2
-LAID_BY_VECTOR = 128
+RUNS = ((0, 192), (192, 352), (352, HALF))
 
 PIECE = 128
 GELU_GROUPS = (256, 256, 256, 128, 128)
 
 TARGET_HALVES = ((0, V // 2), (V // 2, V))
+LAST_PARTS = ((0, 128), (128, 384), (384, V))
 
 
 def tile_picked_median_gelu_e_kernel(
@@ -72,7 +73,6 @@ def tile_picked_median_gelu_e_kernel(
             for d, pos in enumerate((pos1, pos2, pos3)):
                 nc.sync.dma_start(places[d][:], pos)
 
-        quarter = HALF // 2
         for j0, j1 in LOADS:
             nc.sync.dma_start(out=flat[:, j0 * T : j1 * T], in_=rows[:, j0 * T : j1 * T])
             if j0 == 0:
@@ -86,12 +86,11 @@ def tile_picked_median_gelu_e_kernel(
                     nc.vector.tensor_copy(grouped[1][:, :, j], plane.indirect(picks_of(HALF, S)))
                     continue
                 picked = keep.tile([P, HALF], F32, name=f"picked{j}")
-                for s0 in (0, quarter):
-                    nc.scalar.activation(
-                        picked[:, s0 : s0 + quarter], plane.indirect(picks_of(HALF + s0, HALF + s0 + quarter)), ACT.Copy
-                    )
-                nc.vector.tensor_copy(grouped[1][:, 0:LAID_BY_VECTOR, j], picked[:, 0:LAID_BY_VECTOR])
-                for s0, s1 in ((LAID_BY_VECTOR, quarter), (quarter, HALF)):
+                for s0, s1 in RUNS:
+                    nc.scalar.activation(picked[:, s0:s1], plane.indirect(picks_of(HALF + s0, HALF + s1)), ACT.Copy)
+                s0, s1 = RUNS[0]
+                nc.vector.tensor_copy(grouped[1][:, s0:s1, j], picked[:, s0:s1])
+                for s0, s1 in RUNS[1:]:
                     nc.scalar.copy(grouped[1][:, s0:s1, j], picked[:, s0:s1])
 
         def product(m, c0, width, acc):
@@ -162,14 +161,19 @@ def tile_picked_median_gelu_e_kernel(
         for v0, v1 in TARGET_HALVES:
             on_scalar_engine(a[1], 1, 0, v0, v1)
             on_scalar_engine(b[1], 1, 1, v0, v1)
-        for v0, v1 in TARGET_HALVES:
+        for v0, v1 in LAST_PARTS:
             on_scalar_engine(c[1], 1, 2, v0, v1)
         bounds(1, *TARGET_HALVES[0])
         finish(0, 0, V)
         store(0, 0, V)
         bounds(1, *TARGET_HALVES[1])
-        for v0, v1 in TARGET_HALVES:
-            cap(1, v0, v1)
-        for v0, v1 in TARGET_HALVES:
-            finish(1, v0, v1)
-            store(1, v0, v1)
+        first, second, third = LAST_PARTS
+        cap(1, *first)
+        cap(1, *second)
+        finish(1, *first)
+        store(1, *first)
+        cap(1, *third)
+        finish(1, *second)
+        store(1, *second)
+        finish(1, *third)
+        store(1, *third)

@@ -73,6 +73,7 @@ def tile_picked_median_gelu_e_kernel(
             for d, pos in enumerate((pos1, pos2, pos3)):
                 nc.sync.dma_start(places[d][:], pos)
 
+        early = keep.tile([P, SHARED, HALF], F32, name="early")
         for j0, j1 in LOADS:
             nc.sync.dma_start(out=flat[:, j0 * T : j1 * T], in_=rows[:, j0 * T : j1 * T])
             if j0 == 0:
@@ -83,7 +84,9 @@ def tile_picked_median_gelu_e_kernel(
                 plane = flat[:, j * T : (j + 1) * T]
                 nc.vector.tensor_copy(grouped[0][:, :, j], plane.indirect(picks_of(0, HALF)))
                 if j < SHARED:
-                    nc.vector.tensor_copy(grouped[1][:, :, j], plane.indirect(picks_of(HALF, S)))
+                    nc.scalar.activation(early[:, j, :], plane.indirect(picks_of(HALF, S)), ACT.Copy)
+                    if j == SHARED - 1:
+                        nc.vector.tensor_copy(grouped[1][:, :, 0:SHARED], early[:].rearrange("p j s -> p s j"))
                     continue
                 picked = keep.tile([P, HALF], F32, name=f"picked{j}")
                 for s0, s1 in RUNS:

@@ -28,8 +28,7 @@ LOADS = ((0, 2), (2, 3), (3, 4))
 SHARED = 2
 RUNS = ((0, 192), (192, 352), (352, HALF))
 
-PIECE = 128
-GELU_GROUPS = (256, 256, 256, 128, 128)
+GELU_GROUPS = ((256,), (256,), (128, 128), (128,), (128,))
 
 TARGET_HALVES = ((0, V // 2), (V // 2, V))
 LAST_PARTS = ((0, 128), (128, 384), (384, V))
@@ -111,16 +110,18 @@ def tile_picked_median_gelu_e_kernel(
             return psum.tile([P, BANK], F32, name=tag, tag=tag)
 
         g0 = 0
-        for i, width in enumerate(GELU_GROUPS):
+        for i, pieces in enumerate(GELU_GROUPS):
             acc = bank(f"acc{i}")
-            for c0 in range(g0, g0 + width, PIECE):
+            width, c0 = sum(pieces), g0
+            for piece in pieces:
                 h, s0 = divmod(c0, HALF)
                 nc.vector.quantize_mx(
-                    out=codes[:, c0 : c0 + PIECE].bitcast(FP8X4),
-                    scales=scales[:, c0 : c0 + PIECE],
-                    in_=grouped[h][:, s0 : s0 + PIECE, :].rearrange("p s j -> p (s j)"),
+                    out=codes[:, c0 : c0 + piece].bitcast(FP8X4),
+                    scales=scales[:, c0 : c0 + piece],
+                    in_=grouped[h][:, s0 : s0 + piece, :].rearrange("p s j -> p (s j)"),
                 )
-                product(0, c0, PIECE, acc[:, c0 - g0 : c0 - g0 + PIECE])
+                product(0, c0, piece, acc[:, c0 - g0 : c0 - g0 + piece])
+                c0 = c0 + piece
             nc.scalar.activation(y[0][:, g0 : g0 + width], acc[:, 0:width], ACT.Gelu_apprx_tanh)
             g0 = g0 + width
         for h in range(2):
@@ -158,7 +159,8 @@ def tile_picked_median_gelu_e_kernel(
 
         on_vector(a[0], 0, 0, 0, V)
         on_scalar_engine(b[0], 0, 1, 0, V)
-        on_vector(c[0], 0, 2, 0, V)
+        on_vector(c[0], 0, 2, 0, V - 128)
+        on_scalar_engine(c[0], 0, 2, V - 128, V)
         bounds(0, 0, V)
         cap(0, 0, V)
         for v0, v1 in TARGET_HALVES:

@@ -27,6 +27,8 @@ HALF = S // 2
 LOADS = ((0, 2), (2, 3), (3, 4))
 SHARED = 2
 RUNS = ((0, 192), (192, 352), (352, HALF))
+LAID_BY_VECTOR = ((0, 192), (192, 256))
+LAID_BY_SCALAR = ((256, 352), (352, HALF))
 
 GELU_GROUPS = ((256,), (256,), (128, 128), (128,), (128,))
 
@@ -90,9 +92,9 @@ def tile_picked_median_gelu_e_kernel(
                 picked = keep.tile([P, HALF], F32, name=f"picked{j}")
                 for s0, s1 in RUNS:
                     nc.scalar.activation(picked[:, s0:s1], plane.indirect(picks_of(HALF + s0, HALF + s1)), ACT.Copy)
-                s0, s1 = RUNS[0]
-                nc.vector.tensor_copy(grouped[1][:, s0:s1, j], picked[:, s0:s1])
-                for s0, s1 in RUNS[1:]:
+                for s0, s1 in LAID_BY_VECTOR:
+                    nc.vector.tensor_copy(grouped[1][:, s0:s1, j], picked[:, s0:s1])
+                for s0, s1 in LAID_BY_SCALAR:
                     nc.scalar.copy(grouped[1][:, s0:s1, j], picked[:, s0:s1])
 
         def product(m, c0, width, acc):
@@ -124,10 +126,11 @@ def tile_picked_median_gelu_e_kernel(
                 c0 = c0 + piece
             nc.scalar.activation(y[0][:, g0 : g0 + width], acc[:, 0:width], ACT.Gelu_apprx_tanh)
             g0 = g0 + width
-        for h in range(2):
-            acc = bank(f"acc{len(GELU_GROUPS) - 1 - h}")
-            product(1, h * HALF, HALF, acc[:])
-            nc.scalar.activation(y[1][:, h * HALF : (h + 1) * HALF], acc[:], ACT.Gelu_apprx_tanh)
+        last = len(GELU_GROUPS) - 1
+        for c0, c1, tag in ((S - 256, S, last + 1), (HALF, S - 256, last - 1), (0, HALF, last)):
+            acc = bank(f"acc{tag}")
+            product(1, c0, c1 - c0, acc[:, 0 : c1 - c0])
+            nc.scalar.activation(y[1][:, c0:c1], acc[:, 0 : c1 - c0], ACT.Gelu_apprx_tanh)
 
         def fetch(m, d, v0, v1):
             return y[m][:].indirect(places[d][:, v0 // LIST_COLUMN : v1 // LIST_COLUMN])

@@ -26,9 +26,9 @@ HALF = S // 2
 
 LOADS = ((0, 2), (2, 3), (3, 4))
 SHARED = 2
-RUNS = ((0, 192), (192, 352), (352, HALF))
-LAID_BY_VECTOR = ((0, 192), (192, 256))
-LAID_BY_SCALAR = ((256, 352), (352, HALF))
+RUNS = ((0, 256), (256, 384), (384, HALF))
+LAID_BY_GPSIMD = ((0, 256),)
+LAID_BY_SCALAR = ((256, 384), (384, HALF))
 
 GELU_GROUPS = ((256,), (256,), (128, 128), (128,), (128,))
 
@@ -87,13 +87,15 @@ def tile_picked_median_gelu_e_kernel(
                 if j < SHARED:
                     nc.scalar.activation(early[:, j, :], plane.indirect(picks_of(HALF, S)), ACT.Copy)
                     if j == SHARED - 1:
-                        nc.vector.tensor_copy(grouped[1][:, :, 0:SHARED], early[:].rearrange("p j s -> p s j"))
+                        pairs = early[:].rearrange("p j s -> p s j")
+                        nc.gpsimd.tensor_copy(grouped[1][:, 0:256, 0:SHARED], pairs[:, 0:256, :])
+                        nc.vector.tensor_copy(grouped[1][:, 256:HALF, 0:SHARED], pairs[:, 256:HALF, :])
                     continue
                 picked = keep.tile([P, HALF], F32, name=f"picked{j}")
                 for s0, s1 in RUNS:
                     nc.scalar.activation(picked[:, s0:s1], plane.indirect(picks_of(HALF + s0, HALF + s1)), ACT.Copy)
-                for s0, s1 in LAID_BY_VECTOR:
-                    nc.vector.tensor_copy(grouped[1][:, s0:s1, j], picked[:, s0:s1])
+                for s0, s1 in LAID_BY_GPSIMD:
+                    nc.gpsimd.tensor_copy(grouped[1][:, s0:s1, j], picked[:, s0:s1])
                 for s0, s1 in LAID_BY_SCALAR:
                     nc.scalar.copy(grouped[1][:, s0:s1, j], picked[:, s0:s1])
 

@@ -26,11 +26,10 @@ HALF = S // 2
 
 LOADS = ((0, 2), (2, 3), (3, 4))
 SHARED = 2
-RUNS = ((0, 256), (256, 384), (384, HALF))
-LAID_BY_GPSIMD = ((0, 256),)
-LAID_BY_SCALAR = ((256, 384), (384, HALF))
+RUN = 128
+RUNS_ON_GPSIMD = 2
 
-GELU_GROUPS = ((256,), (256,), (128, 128), (128,), (128,))
+GELU_GROUPS = (((512, 640),), ((0, 256),), ((256, 512),), ((640, 768), (768, 896)), ((896, S),))
 
 TARGET_HALVES = ((0, V // 2), (V // 2, V))
 LAST_PARTS = ((0, 128), (128, 384), (384, V))
@@ -51,7 +50,6 @@ def tile_picked_median_gelu_e_kernel(
         w_words = keep.tile([P, 2 * N], U8, name="w_words", align_bytes=64)
         w_scales = keep.tile([P, N], U8, name="w_scales", align_bytes=64)
         grouped = [keep.tile([P, HALF, PACK], BF16, name=f"grouped{h}", align_bytes=64) for h in range(2)]
-        codes = keep.tile([P, S], U32, name="codes", align_bytes=64)
         scales = keep.tile([P, S], U8, name="scales", align_bytes=64)
         y = [keep.tile([P, S], F32, name=f"y{m}") for m in range(N // P)]
 
@@ -91,13 +89,17 @@ def tile_picked_median_gelu_e_kernel(
                         nc.gpsimd.tensor_copy(grouped[1][:, 0:256, 0:SHARED], pairs[:, 0:256, :])
                         nc.vector.tensor_copy(grouped[1][:, 256:HALF, 0:SHARED], pairs[:, 256:HALF, :])
                     continue
-                picked = keep.tile([P, HALF], F32, name=f"picked{j}")
-                for s0, s1 in RUNS:
-                    nc.scalar.activation(picked[:, s0:s1], plane.indirect(picks_of(HALF + s0, HALF + s1)), ACT.Copy)
-                for s0, s1 in LAID_BY_GPSIMD:
-                    nc.gpsimd.tensor_copy(grouped[1][:, s0:s1, j], picked[:, s0:s1])
-                for s0, s1 in LAID_BY_SCALAR:
-                    nc.scalar.copy(grouped[1][:, s0:s1, j], picked[:, s0:s1])
+                runs = []
+                for s0 in range(0, HALF, RUN):
+                    tag = "codes" if (j, s0) == (PACK - 1, 0) else f"run{j}_{s0}"
+                    run = keep.tile([P, RUN], F32, name=f"run{j}_{s0}", tag=tag, align_bytes=64)
+                    nc.scalar.activation(run[:], plane.indirect(picks_of(HALF + s0, HALF + s0 + RUN)), ACT.Copy)
+                    runs.append(run)
+                for i, run in enumerate(runs):
+                    lay = nc.gpsimd.tensor_copy if i < RUNS_ON_GPSIMD else nc.scalar.copy
+                    lay(grouped[1][:, i * RUN : (i + 1) * RUN, j], run[:])
+
+        codes = keep.tile([P, S], U32, name="codes", tag="codes", align_bytes=64)
 
         def product(m, c0, width, acc):
             nc.tensor.matmul_mx(
@@ -113,21 +115,18 @@ def tile_picked_median_gelu_e_kernel(
         def bank(tag):
             return psum.tile([P, BANK], F32, name=tag, tag=tag)
 
-        g0 = 0
         for i, pieces in enumerate(GELU_GROUPS):
             acc = bank(f"acc{i}")
-            width, c0 = sum(pieces), g0
-            for piece in pieces:
+            g0, g1 = pieces[0][0], pieces[-1][1]
+            for c0, c1 in pieces:
                 h, s0 = divmod(c0, HALF)
                 nc.vector.quantize_mx(
-                    out=codes[:, c0 : c0 + piece].bitcast(FP8X4),
-                    scales=scales[:, c0 : c0 + piece],
-                    in_=grouped[h][:, s0 : s0 + piece, :].rearrange("p s j -> p (s j)"),
+                    out=codes[:, c0:c1].bitcast(FP8X4),
+                    scales=scales[:, c0:c1],
+                    in_=grouped[h][:, s0 : s0 + c1 - c0, :].rearrange("p s j -> p (s j)"),
                 )
-                product(0, c0, piece, acc[:, c0 - g0 : c0 - g0 + piece])
-                c0 = c0 + piece
-            nc.scalar.activation(y[0][:, g0 : g0 + width], acc[:, 0:width], ACT.Gelu_apprx_tanh)
-            g0 = g0 + width
+                product(0, c0, c1 - c0, acc[:, c0 - g0 : c1 - g0])
+            nc.scalar.activation(y[0][:, g0:g1], acc[:, 0 : g1 - g0], ACT.Gelu_apprx_tanh)
         last = len(GELU_GROUPS) - 1
         for c0, c1, tag in ((S - 256, S, last + 1), (HALF, S - 256, last - 1), (0, HALF, last)):
             acc = bank(f"acc{tag}")

@@ -24,12 +24,9 @@ QUADRANT = 32
 SCALE_ROWS = 4
 HALF = S // 2
 
-LOADS = ((0, 2), (2, 3), (3, 4))
-SHARED = 2
-RUN = 128
-RUNS_ON_GPSIMD = 2
-
-GELU_GROUPS = (((512, 640),), ((0, 256),), ((256, 512),), ((640, 768), (768, 896)), ((896, S),))
+ON_VECTOR = ((0, 128), (256, 384))
+ON_SCALAR = ((128, 256), (384, 512), (512, 768), (896, S), (768, 896))
+LAID_BY_SCALAR = 896
 
 TARGET_HALVES = ((0, V // 2), (V // 2, V))
 LAST_PARTS = ((0, 128), (128, 384), (384, V))
@@ -44,12 +41,14 @@ def tile_picked_median_gelu_e_kernel(
         psum = ctx.enter_context(tc.psum_pool(name="psum", bufs=1))
 
         rows = xT.rearrange("(p j) t -> p (j t)", j=PACK)
-        flat = keep.tile([P, PACK * T], F32, name="flat")
+        flat = keep.tile([P, (PACK - 1) * T], F32, name="flat")
+        last = keep.tile([P, T], F32, name="last")
         picks = keep.tile([P, S // LIST_COLUMN], U16, name="picks")
         places = [keep.tile([P, V // LIST_COLUMN], U16, name=f"places{d}") for d in range(3)]
         w_words = keep.tile([P, 2 * N], U8, name="w_words", align_bytes=64)
         w_scales = keep.tile([P, N], U8, name="w_scales", align_bytes=64)
-        grouped = [keep.tile([P, HALF, PACK], BF16, name=f"grouped{h}", align_bytes=64) for h in range(2)]
+        grouped = keep.tile([P, S, PACK], BF16, name="grouped", align_bytes=64)
+        codes = keep.tile([P, S], U32, name="codes", align_bytes=64)
         scales = keep.tile([P, S], U8, name="scales", align_bytes=64)
         y = [keep.tile([P, S], F32, name=f"y{m}") for m in range(N // P)]
 
@@ -62,76 +61,82 @@ def tile_picked_median_gelu_e_kernel(
         def picks_of(s0, s1):
             return picks[:, s0 // LIST_COLUMN : s1 // LIST_COLUMN]
 
-        def load_weights_and_places():
-            nc.sync.dma_start(out=w_words[:].bitcast(I32), in_=w1_words[0].bitcast(I32))
-            for r in range(P // QUADRANT):
-                nc.sync.dma_start(
-                    out=w_scales[QUADRANT * r : QUADRANT * r + SCALE_ROWS, :].bitcast(I32),
-                    in_=w1_scales[0, SCALE_ROWS * r : SCALE_ROWS * (r + 1), :].bitcast(I32),
-                )
-            for d, pos in enumerate((pos1, pos2, pos3)):
-                nc.sync.dma_start(places[d][:], pos)
+        nc.sync.dma_start(out=flat[:, 0 : 2 * T], in_=rows[:, 0 : 2 * T])
+        nc.sync.dma_start(picks[:], offs)
+        nc.sync.dma_start(out=flat[:, 2 * T : 3 * T], in_=rows[:, 2 * T : 3 * T])
+        nc.sync.dma_start(out=last[:], in_=rows[:, 3 * T : 4 * T])
+        nc.sync.dma_start(out=w_words[:].bitcast(I32), in_=w1_words[0].bitcast(I32))
+        for r in range(P // QUADRANT):
+            nc.sync.dma_start(
+                out=w_scales[QUADRANT * r : QUADRANT * r + SCALE_ROWS, :].bitcast(I32),
+                in_=w1_scales[0, SCALE_ROWS * r : SCALE_ROWS * (r + 1), :].bitcast(I32),
+            )
+        for d, pos in enumerate((pos1, pos2, pos3)):
+            nc.sync.dma_start(places[d][:], pos)
 
-        early = keep.tile([P, SHARED, HALF], F32, name="early")
-        for j0, j1 in LOADS:
-            nc.sync.dma_start(out=flat[:, j0 * T : j1 * T], in_=rows[:, j0 * T : j1 * T])
-            if j0 == 0:
-                nc.sync.dma_start(picks[:], offs)
-            if j1 == PACK:
-                load_weights_and_places()
-            for j in range(j0, j1):
-                plane = flat[:, j * T : (j + 1) * T]
-                nc.vector.tensor_copy(grouped[0][:, :, j], plane.indirect(picks_of(0, HALF)))
-                if j < SHARED:
-                    nc.scalar.activation(early[:, j, :], plane.indirect(picks_of(HALF, S)), ACT.Copy)
-                    if j == SHARED - 1:
-                        pairs = early[:].rearrange("p j s -> p s j")
-                        nc.gpsimd.tensor_copy(grouped[1][:, 0:256, 0:SHARED], pairs[:, 0:256, :])
-                        nc.vector.tensor_copy(grouped[1][:, 256:HALF, 0:SHARED], pairs[:, 256:HALF, :])
-                    continue
-                runs = []
-                for s0 in range(0, HALF, RUN):
-                    tag = "codes" if (j, s0) == (PACK - 1, 0) else f"run{j}_{s0}"
-                    run = keep.tile([P, RUN], F32, name=f"run{j}_{s0}", tag=tag, align_bytes=64)
-                    nc.scalar.activation(run[:], plane.indirect(picks_of(HALF + s0, HALF + s0 + RUN)), ACT.Copy)
-                    runs.append(run)
-                for i, run in enumerate(runs):
-                    lay = nc.gpsimd.tensor_copy if i < RUNS_ON_GPSIMD else nc.scalar.copy
-                    lay(grouped[1][:, i * RUN : (i + 1) * RUN, j], run[:])
+        early = keep.tile([P, 2, HALF], F32, name="early")
+        for j in range(2):
+            plane = flat[:, j * T : (j + 1) * T]
+            nc.vector.tensor_copy(grouped[:, 0:HALF, j], plane.indirect(picks_of(0, HALF)))
+            nc.scalar.activation(early[:, j, :], plane.indirect(picks_of(HALF, S)), ACT.Copy)
+        pairs = early[:].rearrange("p j s -> p s j")
+        nc.scalar.copy(grouped[:, HALF:LAID_BY_SCALAR, 0:2], pairs[:, 0 : LAID_BY_SCALAR - HALF, :])
+        nc.gpsimd.tensor_copy(grouped[:, LAID_BY_SCALAR:S, 0:2], pairs[:, LAID_BY_SCALAR - HALF : HALF, :])
 
-        codes = keep.tile([P, S], U32, name="codes", tag="codes", align_bytes=64)
+        plane = flat[:, 2 * T : 3 * T]
+        nc.vector.tensor_copy(grouped[:, 0:LAID_BY_SCALAR, 2], plane.indirect(picks_of(0, LAID_BY_SCALAR)))
+        third = keep.tile([P, S - LAID_BY_SCALAR], F32, name="third")
+        nc.scalar.activation(third[:], plane.indirect(picks_of(LAID_BY_SCALAR, S)), ACT.Copy)
+        nc.scalar.copy(grouped[:, LAID_BY_SCALAR:S, 2], third[:])
 
-        def product(m, c0, width, acc):
+        fourth = keep.tile([P, S], BF16, name="fourth")
+        for s0, s1 in ON_VECTOR:
+            nc.vector.tensor_copy(fourth[:, s0:s1], last[:].indirect(picks_of(s0, s1)))
+        for s0, s1 in ON_SCALAR:
+            nc.scalar.activation(fourth[:, s0:s1], last[:].indirect(picks_of(s0, s1)), ACT.Copy)
+
+        def lay(copy, s0, s1):
+            copy(grouped[:, s0:s1, 3], fourth[:, s0:s1])
+
+        def quantise(s0, s1):
+            nc.vector.quantize_mx(
+                out=codes[:, s0:s1].bitcast(FP8X4),
+                scales=scales[:, s0:s1],
+                in_=grouped[:, s0:s1, :].rearrange("p s j -> p (s j)"),
+            )
+
+        def project(m, s0, s1, tag):
+            acc = psum.tile([P, BANK], F32, name=tag, tag=tag)
             nc.tensor.matmul_mx(
-                out=acc,
+                out=acc[:, 0 : s1 - s0],
                 lhsT=w_words[:, 2 * P * m : 2 * P * (m + 1)].bitcast(FP4X4),
                 lhsT_scale=w_scales[:, P * m : P * (m + 1)],
-                rhs=codes[:, c0 : c0 + width].bitcast(FP8X4),
-                rhs_scale=scales[:, c0 : c0 + width],
+                rhs=codes[:, s0:s1].bitcast(FP8X4),
+                rhs_scale=scales[:, s0:s1],
                 start=True,
                 stop=True,
             )
+            nc.scalar.activation(y[m][:, s0:s1], acc[:, 0 : s1 - s0], ACT.Gelu_apprx_tanh)
 
-        def bank(tag):
-            return psum.tile([P, BANK], F32, name=tag, tag=tag)
-
-        for i, pieces in enumerate(GELU_GROUPS):
-            acc = bank(f"acc{i}")
-            g0, g1 = pieces[0][0], pieces[-1][1]
-            for c0, c1 in pieces:
-                h, s0 = divmod(c0, HALF)
-                nc.vector.quantize_mx(
-                    out=codes[:, c0:c1].bitcast(FP8X4),
-                    scales=scales[:, c0:c1],
-                    in_=grouped[h][:, s0 : s0 + c1 - c0, :].rearrange("p s j -> p (s j)"),
-                )
-                product(0, c0, c1 - c0, acc[:, c0 - g0 : c1 - g0])
-            nc.scalar.activation(y[0][:, g0:g1], acc[:, 0 : g1 - g0], ACT.Gelu_apprx_tanh)
-        last = len(GELU_GROUPS) - 1
-        for c0, c1, tag in ((S - 256, S, last + 1), (HALF, S - 256, last - 1), (0, HALF, last)):
-            acc = bank(f"acc{tag}")
-            product(1, c0, c1 - c0, acc[:, 0 : c1 - c0])
-            nc.scalar.activation(y[1][:, c0:c1], acc[:, 0 : c1 - c0], ACT.Gelu_apprx_tanh)
+        lay(nc.scalar.copy, 896, S)
+        lay(nc.vector.tensor_copy, 0, 256)
+        lay(nc.vector.tensor_copy, 256, 512)
+        quantise(0, 256)
+        project(0, 0, 256, "acc0")
+        project(1, 0, 256, "acc1")
+        lay(nc.vector.tensor_copy, 512, 768)
+        quantise(256, 512)
+        project(0, 256, 512, "acc2")
+        project(1, 256, 512, "acc3")
+        lay(nc.vector.tensor_copy, 768, 896)
+        quantise(512, 768)
+        project(0, 512, 768, "acc4")
+        quantise(896, S)
+        project(0, 896, S, "acc5")
+        quantise(768, 896)
+        project(0, 768, 896, "acc6")
+        project(1, 768, S, "acc7")
+        project(1, 512, 768, "acc5")
 
         def fetch(m, d, v0, v1):
             return y[m][:].indirect(places[d][:, v0 // LIST_COLUMN : v1 // LIST_COLUMN])
@@ -163,8 +168,8 @@ def tile_picked_median_gelu_e_kernel(
 
         on_vector(a[0], 0, 0, 0, V)
         on_scalar_engine(b[0], 0, 1, 0, V)
-        on_vector(c[0], 0, 2, 0, V - 128)
-        on_scalar_engine(c[0], 0, 2, V - 128, V)
+        on_vector(c[0], 0, 2, 0, V - 64)
+        on_scalar_engine(c[0], 0, 2, V - 64, V)
         bounds(0, 0, V)
         cap(0, 0, V)
         for v0, v1 in TARGET_HALVES:

@@ -24,9 +24,10 @@ QUADRANT = 32
 SCALE_ROWS = 4
 HALF = S // 2
 
-ON_VECTOR = ((0, 128), (256, 384))
-ON_SCALAR = ((128, 256), (384, 512), (512, 768), (896, S), (768, 896))
-LAID_BY_SCALAR = 896
+RUNS = ((0, 128), (128, 256), (256, 384), (384, HALF))
+LAID_BY_GPSIMD = ((0, 128), (128, 192))
+LAID_BY_VECTOR = ((192, 256),)
+LAID_BY_SCALAR = ((256, 384), (384, HALF))
 
 TARGET_HALVES = ((0, V // 2), (V // 2, V))
 LAST_PARTS = ((0, 128), (128, 384), (384, V))
@@ -47,7 +48,8 @@ def tile_picked_median_gelu_e_kernel(
         places = [keep.tile([P, V // LIST_COLUMN], U16, name=f"places{d}") for d in range(3)]
         w_words = keep.tile([P, 2 * N], U8, name="w_words", align_bytes=64)
         w_scales = keep.tile([P, N], U8, name="w_scales", align_bytes=64)
-        grouped = keep.tile([P, S, PACK], BF16, name="grouped", align_bytes=64)
+        pairs = keep.tile([P, 2, HALF, 2], BF16, name="pairs")
+        grouped = keep.tile([P, HALF, PACK], BF16, name="grouped", align_bytes=64)
         codes = keep.tile([P, S], U32, name="codes", align_bytes=64)
         scales = keep.tile([P, S], U8, name="scales", align_bytes=64)
         y = [keep.tile([P, S], F32, name=f"y{m}") for m in range(N // P)]
@@ -75,34 +77,49 @@ def tile_picked_median_gelu_e_kernel(
             nc.sync.dma_start(places[d][:], pos)
 
         early = keep.tile([P, 2, HALF], F32, name="early")
-        for j in range(2):
-            plane = flat[:, j * T : (j + 1) * T]
-            nc.vector.tensor_copy(grouped[:, 0:HALF, j], plane.indirect(picks_of(0, HALF)))
-            nc.scalar.activation(early[:, j, :], plane.indirect(picks_of(HALF, S)), ACT.Copy)
-        pairs = early[:].rearrange("p j s -> p s j")
-        nc.scalar.copy(grouped[:, HALF:LAID_BY_SCALAR, 0:2], pairs[:, 0 : LAID_BY_SCALAR - HALF, :])
-        nc.gpsimd.tensor_copy(grouped[:, LAID_BY_SCALAR:S, 0:2], pairs[:, LAID_BY_SCALAR - HALF : HALF, :])
+        for j in range(PACK):
+            plane = last[:] if j == PACK - 1 else flat[:, j * T : (j + 1) * T]
+            nc.vector.tensor_copy(pairs[:, j // 2, :, j % 2], plane.indirect(picks_of(0, HALF)))
+            if j < 2:
+                nc.scalar.activation(early[:, j, :], plane.indirect(picks_of(HALF, S)), ACT.Copy)
+                if j == 1:
+                    both = early[:].rearrange("p j s -> p s j")
+                    nc.gpsimd.tensor_copy(grouped[:, 0:192, 0:2], both[:, 0:192, :])
+                    nc.scalar.copy(grouped[:, 192:HALF, 0:2], both[:, 192:HALF, :])
+                continue
+            runs = []
+            for i, (s0, s1) in enumerate(RUNS):
+                tag = ("woven0", "woven1", "last2", "last3")[i] if j == PACK - 1 else f"run{i}"
+                run = keep.tile([P, s1 - s0], F32, name=f"run{j}_{i}", tag=tag, align_bytes=64)
+                nc.scalar.activation(run[:], plane.indirect(picks_of(HALF + s0, HALF + s1)), ACT.Copy)
+                runs.append(run)
+            for copy, parts in (
+                (nc.gpsimd.tensor_copy, LAID_BY_GPSIMD),
+                (nc.vector.tensor_copy, LAID_BY_VECTOR),
+                (nc.scalar.copy, LAID_BY_SCALAR),
+            ):
+                for s0, s1 in parts:
+                    i = max(n for n, (r0, r1) in enumerate(RUNS) if r0 <= s0)
+                    copy(grouped[:, s0:s1, j], runs[i][:, s0 - RUNS[i][0] : s1 - RUNS[i][0]])
 
-        plane = flat[:, 2 * T : 3 * T]
-        nc.vector.tensor_copy(grouped[:, 0:LAID_BY_SCALAR, 2], plane.indirect(picks_of(0, LAID_BY_SCALAR)))
-        third = keep.tile([P, S - LAID_BY_SCALAR], F32, name="third")
-        nc.scalar.activation(third[:], plane.indirect(picks_of(LAID_BY_SCALAR, S)), ACT.Copy)
-        nc.scalar.copy(grouped[:, LAID_BY_SCALAR:S, 2], third[:])
+        words = pairs[:].rearrange("p u s e -> p u (s e)").bitcast(I32)
+        woven = [keep.tile([P, 256 * PACK], BF16, name=f"woven{i}", tag=f"woven{i}", align_bytes=64) for i in range(2)]
 
-        fourth = keep.tile([P, S], BF16, name="fourth")
-        for s0, s1 in ON_VECTOR:
-            nc.vector.tensor_copy(fourth[:, s0:s1], last[:].indirect(picks_of(s0, s1)))
-        for s0, s1 in ON_SCALAR:
-            nc.scalar.activation(fourth[:, s0:s1], last[:].indirect(picks_of(s0, s1)), ACT.Copy)
-
-        def lay(copy, s0, s1):
-            copy(grouped[:, s0:s1, 3], fourth[:, s0:s1])
+        def weave(i):
+            nc.vector.tensor_copy(
+                woven[i][:].bitcast(I32).rearrange("p (s u) -> p s u", u=2),
+                words[:, :, 256 * i : 256 * (i + 1)].rearrange("p u s -> p s u"),
+            )
 
         def quantise(s0, s1):
+            if s0 < HALF:
+                values = woven[s0 // 256][:, s0 % 256 * PACK : (s0 % 256 + s1 - s0) * PACK]
+            else:
+                values = grouped[:, s0 - HALF : s1 - HALF, :].rearrange("p s j -> p (s j)")
             nc.vector.quantize_mx(
                 out=codes[:, s0:s1].bitcast(FP8X4),
                 scales=scales[:, s0:s1],
-                in_=grouped[:, s0:s1, :].rearrange("p s j -> p (s j)"),
+                in_=values,
             )
 
         def project(m, s0, s1, tag):
@@ -118,25 +135,23 @@ def tile_picked_median_gelu_e_kernel(
             )
             nc.scalar.activation(y[m][:, s0:s1], acc[:, 0 : s1 - s0], ACT.Gelu_apprx_tanh)
 
-        lay(nc.scalar.copy, 896, S)
-        lay(nc.vector.tensor_copy, 0, 256)
-        lay(nc.vector.tensor_copy, 256, 512)
+        quantise(512, 640)
+        project(0, 512, 640, "acc0")
+        weave(0)
+        quantise(640, 768)
+        project(0, 640, 768, "acc2")
+        project(1, 512, 768, "acc3")
+        weave(1)
         quantise(0, 256)
-        project(0, 0, 256, "acc0")
-        project(1, 0, 256, "acc1")
-        lay(nc.vector.tensor_copy, 512, 768)
-        quantise(256, 512)
-        project(0, 256, 512, "acc2")
-        project(1, 256, 512, "acc3")
-        lay(nc.vector.tensor_copy, 768, 896)
-        quantise(512, 768)
-        project(0, 512, 768, "acc4")
-        quantise(896, S)
-        project(0, 896, S, "acc5")
+        project(0, 0, 256, "acc4")
         quantise(768, 896)
-        project(0, 768, 896, "acc6")
-        project(1, 768, S, "acc7")
-        project(1, 512, 768, "acc5")
+        project(0, 768, 896, "acc5")
+        quantise(256, 512)
+        project(0, 256, 512, "acc6")
+        quantise(896, S)
+        project(0, 896, S, "acc7")
+        project(1, 768, S, "acc0")
+        project(1, 0, 512, "acc6")
 
         def fetch(m, d, v0, v1):
             return y[m][:].indirect(places[d][:, v0 // LIST_COLUMN : v1 // LIST_COLUMN])
@@ -168,8 +183,8 @@ def tile_picked_median_gelu_e_kernel(
 
         on_vector(a[0], 0, 0, 0, V)
         on_scalar_engine(b[0], 0, 1, 0, V)
-        on_vector(c[0], 0, 2, 0, V - 64)
-        on_scalar_engine(c[0], 0, 2, V - 64, V)
+        on_vector(c[0], 0, 2, 0, V - 96)
+        on_scalar_engine(c[0], 0, 2, V - 96, V)
         bounds(0, 0, V)
         cap(0, 0, V)
         for v0, v1 in TARGET_HALVES:

@@ -144,10 +144,10 @@ def tile_picked_median_gelu_e_kernel(
         weave(1)
         quantise(0, 256)
         project(0, 0, 256, "acc4")
-        quantise(768, 896)
-        project(0, 768, 896, "acc5")
         quantise(256, 512)
-        project(0, 256, 512, "acc6")
+        project(0, 256, 512, "acc5")
+        quantise(768, 896)
+        project(0, 768, 896, "acc6")
         quantise(896, S)
         project(0, 896, S, "acc7")
         project(1, 768, S, "acc0")
@@ -182,9 +182,9 @@ def tile_picked_median_gelu_e_kernel(
             nc.sync.dma_start(out=out[m * P : (m + 1) * P, v0:v1], in_=median[m][:, v0:v1])
 
         on_vector(a[0], 0, 0, 0, V)
-        on_scalar_engine(b[0], 0, 1, 0, V)
-        on_vector(c[0], 0, 2, 0, V - 96)
-        on_scalar_engine(c[0], 0, 2, V - 96, V)
+        on_scalar_engine(b[0], 0, 1, 0, V - 128)
+        on_scalar_engine(b[0], 0, 1, V - 128, V)
+        on_vector(c[0], 0, 2, 0, V)
         bounds(0, 0, V)
         cap(0, 0, V)
         for v0, v1 in TARGET_HALVES:

@@ -25,12 +25,12 @@ SCALE_ROWS = 4
 HALF = S // 2
 
 RUNS = ((0, 128), (128, 256), (256, 384), (384, HALF))
-LAID_BY_GPSIMD = ((0, 128), (128, 192))
-LAID_BY_VECTOR = ((192, 256),)
+LAID_BY_GPSIMD = ((0, 128),)
+LAID_BY_VECTOR = ((128, 256),)
 LAID_BY_SCALAR = ((256, 384), (384, HALF))
 
 TARGET_HALVES = ((0, V // 2), (V // 2, V))
-LAST_PARTS = ((0, 128), (128, 384), (384, V))
+LAST_PARTS = ((0, 192), (192, 384), (384, V))
 
 
 def tile_picked_median_gelu_e_kernel(
@@ -84,12 +84,12 @@ def tile_picked_median_gelu_e_kernel(
                 nc.scalar.activation(early[:, j, :], plane.indirect(picks_of(HALF, S)), ACT.Copy)
                 if j == 1:
                     both = early[:].rearrange("p j s -> p s j")
-                    nc.gpsimd.tensor_copy(grouped[:, 0:192, 0:2], both[:, 0:192, :])
-                    nc.scalar.copy(grouped[:, 192:HALF, 0:2], both[:, 192:HALF, :])
+                    nc.gpsimd.tensor_copy(grouped[:, 0:128, 0:2], both[:, 0:128, :])
+                    nc.scalar.copy(grouped[:, 128:HALF, 0:2], both[:, 128:HALF, :])
                 continue
             runs = []
             for i, (s0, s1) in enumerate(RUNS):
-                tag = ("woven0", "woven1", "last2", "last3")[i] if j == PACK - 1 else f"run{i}"
+                tag = "woven" if (j, i) == (PACK - 1, 0) else f"run{j}_{i}"
                 run = keep.tile([P, s1 - s0], F32, name=f"run{j}_{i}", tag=tag, align_bytes=64)
                 nc.scalar.activation(run[:], plane.indirect(picks_of(HALF + s0, HALF + s1)), ACT.Copy)
                 runs.append(run)
@@ -103,17 +103,17 @@ def tile_picked_median_gelu_e_kernel(
                     copy(grouped[:, s0:s1, j], runs[i][:, s0 - RUNS[i][0] : s1 - RUNS[i][0]])
 
         words = pairs[:].rearrange("p u s e -> p u (s e)").bitcast(I32)
-        woven = [keep.tile([P, 256 * PACK], BF16, name=f"woven{i}", tag=f"woven{i}", align_bytes=64) for i in range(2)]
+        woven = keep.tile([P, HALF * PACK], BF16, name="woven", tag="woven", align_bytes=64)
 
         def weave(i):
             nc.vector.tensor_copy(
-                woven[i][:].bitcast(I32).rearrange("p (s u) -> p s u", u=2),
+                woven[:, 256 * PACK * i : 256 * PACK * (i + 1)].bitcast(I32).rearrange("p (s u) -> p s u", u=2),
                 words[:, :, 256 * i : 256 * (i + 1)].rearrange("p u s -> p s u"),
             )
 
         def quantise(s0, s1):
             if s0 < HALF:
-                values = woven[s0 // 256][:, s0 % 256 * PACK : (s0 % 256 + s1 - s0) * PACK]
+                values = woven[:, s0 * PACK : s1 * PACK]
             else:
                 values = grouped[:, s0 - HALF : s1 - HALF, :].rearrange("p s j -> p (s j)")
             nc.vector.quantize_mx(

@@ -29,6 +29,8 @@ LAID_BY_GPSIMD = ((0, 128),)
 LAID_BY_VECTOR = ((128, 256),)
 LAID_BY_SCALAR = ((256, 384), (384, HALF))
 
+EXACT = 224
+
 TARGET_HALVES = ((0, V // 2), (V // 2, V))
 LAST_PARTS = ((0, 192), (192, 384), (384, V))
 
@@ -181,21 +183,31 @@ def tile_picked_median_gelu_e_kernel(
         def store(m, v0, v1):
             nc.sync.dma_start(out=out[m * P : (m + 1) * P, v0:v1], in_=median[m][:, v0:v1])
 
-        on_vector(a[0], 0, 0, 0, V)
-        on_scalar_engine(b[0], 0, 1, 0, V - 128)
-        on_scalar_engine(b[0], 0, 1, V - 128, V)
-        on_vector(c[0], 0, 2, 0, V)
-        bounds(0, 0, V)
-        cap(0, 0, V)
+        def step(dst, in0, in1, op, m, v0, v1):
+            nc.vector.tensor_tensor(dst[m][:, v0:v1], in0[m][:, v0:v1], in1[m][:, v0:v1], op)
+
+        rest = slice(EXACT, V)
+        on_vector(a[0], 0, 0, 0, EXACT)
+        on_scalar_engine(a[0], 0, 0, EXACT, V)
+        on_vector(c[0], 0, 2, 0, EXACT)
+        nc.vector.tensor_tensor(b[0][:, rest], fetch(0, 1, EXACT, V), a[0][:, rest], ALU.subtract)
+        nc.vector.tensor_tensor(c[0][:, rest], fetch(0, 2, EXACT, V), a[0][:, rest], ALU.subtract)
+        on_scalar_engine(b[0], 0, 1, 0, EXACT)
         for v0, v1 in TARGET_HALVES:
             on_scalar_engine(a[1], 1, 0, v0, v1)
             on_scalar_engine(b[1], 1, 1, v0, v1)
         for v0, v1 in LAST_PARTS:
             on_scalar_engine(c[1], 1, 2, v0, v1)
-        bounds(1, *TARGET_HALVES[0])
-        finish(0, 0, V)
+        step(high, a, b, ALU.max, 0, 0, EXACT)
+        step(low, a, b, ALU.min, 0, 0, EXACT)
+        nc.vector.scalar_tensor_tensor(capped[0][:, rest], b[0][:, rest], 0.0, c[0][:, rest], ALU.max, ALU.min)
+        cap(0, 0, EXACT)
+        nc.vector.scalar_tensor_tensor(low[0][:, rest], b[0][:, rest], 0.0, capped[0][:, rest], ALU.min, ALU.max)
+        finish(0, 0, EXACT)
+        step(median, low, a, ALU.add, 0, EXACT, V)
         store(0, 0, V)
-        bounds(1, *TARGET_HALVES[1])
+        for v0, v1 in TARGET_HALVES:
+            bounds(1, v0, v1)
         first, second, third = LAST_PARTS
         cap(1, *first)
         cap(1, *second)

@@ -29,7 +29,8 @@ LAID_BY_GPSIMD = ((0, 128),)
 LAID_BY_VECTOR = ((128, 256),)
 LAID_BY_SCALAR = ((256, 384), (384, HALF))
 
-EXACT = 224
+EXACT = 192
+OWN_A = 256
 
 TARGET_HALVES = ((0, V // 2), (V // 2, V))
 LAST_PARTS = ((0, 192), (192, 384), (384, V))
@@ -187,8 +188,8 @@ def tile_picked_median_gelu_e_kernel(
             nc.vector.tensor_tensor(dst[m][:, v0:v1], in0[m][:, v0:v1], in1[m][:, v0:v1], op)
 
         rest = slice(EXACT, V)
-        on_vector(a[0], 0, 0, 0, EXACT)
-        on_scalar_engine(a[0], 0, 0, EXACT, V)
+        on_vector(a[0], 0, 0, 0, OWN_A)
+        on_scalar_engine(a[0], 0, 0, OWN_A, V)
         on_vector(c[0], 0, 2, 0, EXACT)
         nc.vector.tensor_tensor(b[0][:, rest], fetch(0, 1, EXACT, V), a[0][:, rest], ALU.subtract)
         nc.vector.tensor_tensor(c[0][:, rest], fetch(0, 2, EXACT, V), a[0][:, rest], ALU.subtract)

@@ -154,7 +154,6 @@ def tile_picked_median_gelu_e_kernel(
         quantise(896, S)
         project(0, 896, S, "acc7")
         project(1, 768, S, "acc0")
-        project(1, 0, 512, "acc6")
 
         def fetch(m, d, v0, v1):
             return y[m][:].indirect(places[d][:, v0 // LIST_COLUMN : v1 // LIST_COLUMN])
@@ -190,6 +189,7 @@ def tile_picked_median_gelu_e_kernel(
         rest = slice(EXACT, V)
         on_vector(a[0], 0, 0, 0, OWN_A)
         on_scalar_engine(a[0], 0, 0, OWN_A, V)
+        project(1, 0, HALF, "acc5")
         on_vector(c[0], 0, 2, 0, EXACT)
         nc.vector.tensor_tensor(b[0][:, rest], fetch(0, 1, EXACT, V), a[0][:, rest], ALU.subtract)
         nc.vector.tensor_tensor(c[0][:, rest], fetch(0, 2, EXACT, V), a[0][:, rest], ALU.subtract)

@@ -149,10 +149,8 @@ def tile_picked_median_gelu_e_kernel(
         project(0, 0, 256, "acc4")
         quantise(256, 512)
         project(0, 256, 512, "acc5")
-        quantise(768, 896)
-        project(0, 768, 896, "acc6")
-        quantise(896, S)
-        project(0, 896, S, "acc7")
+        quantise(768, S)
+        project(0, 768, S, "acc6")
         project(1, 768, S, "acc0")
 
         def fetch(m, d, v0, v1):

@@ -24,8 +24,8 @@ QUADRANT = 32
 SCALE_ROWS = 4
 HALF = S // 2
 
-RUNS = ((0, 128), (128, 256), (256, 384), (384, HALF))
-LAID_BY_GPSIMD = ((0, 128),)
+RUNS = ((0, 64), (64, 128), (128, 256), (256, 384), (384, HALF))
+LAID_BY_GPSIMD = ((0, 64), (64, 128))
 LAID_BY_VECTOR = ((128, 256),)
 LAID_BY_SCALAR = ((256, 384), (384, HALF))
 
@@ -92,7 +92,7 @@ def tile_picked_median_gelu_e_kernel(
                 continue
             runs = []
             for i, (s0, s1) in enumerate(RUNS):
-                tag = "woven" if (j, i) == (PACK - 1, 0) else f"run{j}_{i}"
+                tag = "woven" if (j, i) == (PACK - 1, 1) else f"run{j}_{i}"
                 run = keep.tile([P, s1 - s0], F32, name=f"run{j}_{i}", tag=tag, align_bytes=64)
                 nc.scalar.activation(run[:], plane.indirect(picks_of(HALF + s0, HALF + s1)), ACT.Copy)
                 runs.append(run)

@@ -32,7 +32,7 @@ LAID_BY_SCALAR = ((256, 384), (384, HALF))
 EXACT = 192
 OWN_A = 256
 
-TARGET_HALVES = ((0, V // 2), (V // 2, V))
+TARGET_HALVES = ((0, 192), (192, V))
 LAST_PARTS = ((0, 192), (192, 384), (384, V))
 
 

from contextlib import ExitStack

import concourse.mybir as mybir

K, T, S, V, N = 512, 4096, 1024, 512, 256
FLOPS = 2 * K * N * S

F32 = mybir.dt.float32
BF16 = mybir.dt.bfloat16
I32 = mybir.dt.int32
U32 = mybir.dt.uint32
U16 = mybir.dt.uint16
U8 = mybir.dt.uint8
FP8X4 = mybir.dt.float8_e4m3fn_x4
FP4X4 = mybir.dt.float4_e2m1fn_x4
ALU = mybir.AluOpType
ACT = mybir.ActivationFunctionType

P = 128
PACK = 4
LIST_COLUMN = 16
BANK = 512
QUADRANT = 32
SCALE_ROWS = 4
HALF = S // 2

RUNS = ((0, 64), (64, 128), (128, 256), (256, 384), (384, HALF))
LAID_BY_GPSIMD = ((0, 64), (64, 128))
LAID_BY_VECTOR = ((128, 256),)
LAID_BY_SCALAR = ((256, 384), (384, HALF))

EXACT = 192
OWN_A = 256

TARGET_HALVES = ((0, 192), (192, V))
LAST_PARTS = ((0, 192), (192, 384), (384, V))


def tile_picked_median_gelu_e_kernel(
    tc, xT, w1_words, w1_scales, offs, pos1, pos2, pos3, out
):
    nc = tc.nc
    with ExitStack() as ctx:
        keep = ctx.enter_context(tc.tile_pool(name="keep", bufs=1))
        psum = ctx.enter_context(tc.psum_pool(name="psum", bufs=1))

        rows = xT.rearrange("(p j) t -> p (j t)", j=PACK)
        flat = keep.tile([P, (PACK - 1) * T], F32, name="flat")
        last = keep.tile([P, T], F32, name="last")
        picks = keep.tile([P, S // LIST_COLUMN], U16, name="picks")
        places = [keep.tile([P, V // LIST_COLUMN], U16, name=f"places{d}") for d in range(3)]
        w_words = keep.tile([P, 2 * N], U8, name="w_words", align_bytes=64)
        w_scales = keep.tile([P, N], U8, name="w_scales", align_bytes=64)
        pairs = keep.tile([P, 2, HALF, 2], BF16, name="pairs")
        grouped = keep.tile([P, HALF, PACK], BF16, name="grouped", align_bytes=64)
        codes = keep.tile([P, S], U32, name="codes", align_bytes=64)
        scales = keep.tile([P, S], U8, name="scales", align_bytes=64)
        y = [keep.tile([P, S], F32, name=f"y{m}") for m in range(N // P)]

        warm = keep.tile([P, 2], F32, name="warm")
        nc.vector.memset(warm[:, 0:1], 0.0)
        nc.scalar.activation(warm[:, 1:2], warm[:, 0:1], ACT.Gelu_apprx_tanh)

        nc.vector.memset(w_scales[:].bitcast(I32), 0)

        def picks_of(s0, s1):
            return picks[:, s0 // LIST_COLUMN : s1 // LIST_COLUMN]

        nc.sync.dma_start(out=flat[:, 0 : 2 * T], in_=rows[:, 0 : 2 * T])
        nc.sync.dma_start(picks[:], offs)
        nc.sync.dma_start(out=flat[:, 2 * T : 3 * T], in_=rows[:, 2 * T : 3 * T])
        nc.sync.dma_start(out=last[:], in_=rows[:, 3 * T : 4 * T])
        nc.sync.dma_start(out=w_words[:].bitcast(I32), in_=w1_words[0].bitcast(I32))
        for r in range(P // QUADRANT):
            nc.sync.dma_start(
                out=w_scales[QUADRANT * r : QUADRANT * r + SCALE_ROWS, :].bitcast(I32),
                in_=w1_scales[0, SCALE_ROWS * r : SCALE_ROWS * (r + 1), :].bitcast(I32),
            )
        for d, pos in enumerate((pos1, pos2, pos3)):
            nc.sync.dma_start(places[d][:], pos)

        early = keep.tile([P, 2, HALF], F32, name="early")
        for j in range(PACK):
            plane = last[:] if j == PACK - 1 else flat[:, j * T : (j + 1) * T]
            nc.vector.tensor_copy(pairs[:, j // 2, :, j % 2], plane.indirect(picks_of(0, HALF)))
            if j < 2:
                nc.scalar.activation(early[:, j, :], plane.indirect(picks_of(HALF, S)), ACT.Copy)
                if j == 1:
                    both = early[:].rearrange("p j s -> p s j")
                    nc.gpsimd.tensor_copy(grouped[:, 0:128, 0:2], both[:, 0:128, :])
                    nc.scalar.copy(grouped[:, 128:HALF, 0:2], both[:, 128:HALF, :])
                continue
            runs = []
            for i, (s0, s1) in enumerate(RUNS):
                tag = "woven" if (j, i) == (PACK - 1, 1) else f"run{j}_{i}"
                run = keep.tile([P, s1 - s0], F32, name=f"run{j}_{i}", tag=tag, align_bytes=64)
                nc.scalar.activation(run[:], plane.indirect(picks_of(HALF + s0, HALF + s1)), ACT.Copy)
                runs.append(run)
            for copy, parts in (
                (nc.gpsimd.tensor_copy, LAID_BY_GPSIMD),
                (nc.vector.tensor_copy, LAID_BY_VECTOR),
                (nc.scalar.copy, LAID_BY_SCALAR),
            ):
                for s0, s1 in parts:
                    i = max(n for n, (r0, r1) in enumerate(RUNS) if r0 <= s0)
                    copy(grouped[:, s0:s1, j], runs[i][:, s0 - RUNS[i][0] : s1 - RUNS[i][0]])

        words = pairs[:].rearrange("p u s e -> p u (s e)").bitcast(I32)
        woven = keep.tile([P, HALF * PACK], BF16, name="woven", tag="woven", align_bytes=64)

        def weave(i):
            nc.vector.tensor_copy(
                woven[:, 256 * PACK * i : 256 * PACK * (i + 1)].bitcast(I32).rearrange("p (s u) -> p s u", u=2),
                words[:, :, 256 * i : 256 * (i + 1)].rearrange("p u s -> p s u"),
            )

        def quantise(s0, s1):
            if s0 < HALF:
                values = woven[:, s0 * PACK : s1 * PACK]
            else:
                values = grouped[:, s0 - HALF : s1 - HALF, :].rearrange("p s j -> p (s j)")
            nc.vector.quantize_mx(
                out=codes[:, s0:s1].bitcast(FP8X4),
                scales=scales[:, s0:s1],
                in_=values,
            )

        def project(m, s0, s1, tag):
            acc = psum.tile([P, BANK], F32, name=tag, tag=tag)
            nc.tensor.matmul_mx(
                out=acc[:, 0 : s1 - s0],
                lhsT=w_words[:, 2 * P * m : 2 * P * (m + 1)].bitcast(FP4X4),
                lhsT_scale=w_scales[:, P * m : P * (m + 1)],
                rhs=codes[:, s0:s1].bitcast(FP8X4),
                rhs_scale=scales[:, s0:s1],
                start=True,
                stop=True,
            )
            nc.scalar.activation(y[m][:, s0:s1], acc[:, 0 : s1 - s0], ACT.Gelu_apprx_tanh)

        quantise(512, 640)
        project(0, 512, 640, "acc0")
        weave(0)
        quantise(640, 768)
        project(0, 640, 768, "acc2")
        project(1, 512, 768, "acc3")
        weave(1)
        quantise(0, 256)
        project(0, 0, 256, "acc4")
        quantise(256, 512)
        project(0, 256, 512, "acc5")
        quantise(768, S)
        project(0, 768, S, "acc6")
        project(1, 768, S, "acc0")

        def fetch(m, d, v0, v1):
            return y[m][:].indirect(places[d][:, v0 // LIST_COLUMN : v1 // LIST_COLUMN])

        def on_vector(dst, m, d, v0, v1):
            nc.vector.tensor_copy(dst[:, v0:v1], fetch(m, d, v0, v1))

        def on_scalar_engine(dst, m, d, v0, v1):
            nc.scalar.activation(dst[:, v0:v1], fetch(m, d, v0, v1), ACT.Copy)

        def tiles_of(name):
            return [keep.tile([P, V], F32, name=f"{name}{m}") for m in range(N // P)]

        a, b, c = tiles_of("a"), tiles_of("b"), tiles_of("c")
        low, high, capped, median = tiles_of("low"), tiles_of("high"), tiles_of("capped"), tiles_of("median")

        def bounds(m, v0, v1):
            nc.vector.tensor_tensor(high[m][:, v0:v1], a[m][:, v0:v1], b[m][:, v0:v1], ALU.max)
            nc.vector.tensor_tensor(low[m][:, v0:v1], a[m][:, v0:v1], b[m][:, v0:v1], ALU.min)

        def cap(m, v0, v1):
            nc.vector.tensor_tensor(capped[m][:, v0:v1], high[m][:, v0:v1], c[m][:, v0:v1], ALU.min)

        def finish(m, v0, v1):
            nc.vector.tensor_tensor(median[m][:, v0:v1], low[m][:, v0:v1], capped[m][:, v0:v1], ALU.max)

        def store(m, v0, v1):
            nc.sync.dma_start(out=out[m * P : (m + 1) * P, v0:v1], in_=median[m][:, v0:v1])

        def step(dst, in0, in1, op, m, v0, v1):
            nc.vector.tensor_tensor(dst[m][:, v0:v1], in0[m][:, v0:v1], in1[m][:, v0:v1], op)

        rest = slice(EXACT, V)
        on_vector(a[0], 0, 0, 0, OWN_A)
        on_scalar_engine(a[0], 0, 0, OWN_A, V)
        project(1, 0, HALF, "acc5")
        on_vector(c[0], 0, 2, 0, EXACT)
        nc.vector.tensor_tensor(b[0][:, rest], fetch(0, 1, EXACT, V), a[0][:, rest], ALU.subtract)
        nc.vector.tensor_tensor(c[0][:, rest], fetch(0, 2, EXACT, V), a[0][:, rest], ALU.subtract)
        on_scalar_engine(b[0], 0, 1, 0, EXACT)
        for v0, v1 in TARGET_HALVES:
            on_scalar_engine(a[1], 1, 0, v0, v1)
            on_scalar_engine(b[1], 1, 1, v0, v1)
        for v0, v1 in LAST_PARTS:
            on_scalar_engine(c[1], 1, 2, v0, v1)
        step(high, a, b, ALU.max, 0, 0, EXACT)
        step(low, a, b, ALU.min, 0, 0, EXACT)
        nc.vector.scalar_tensor_tensor(capped[0][:, rest], b[0][:, rest], 0.0, c[0][:, rest], ALU.max, ALU.min)
        cap(0, 0, EXACT)
        nc.vector.scalar_tensor_tensor(low[0][:, rest], b[0][:, rest], 0.0, capped[0][:, rest], ALU.min, ALU.max)
        finish(0, 0, EXACT)
        step(median, low, a, ALU.add, 0, EXACT, V)
        store(0, 0, V)
        for v0, v1 in TARGET_HALVES:
            bounds(1, v0, v1)
        first, second, third = LAST_PARTS
        cap(1, *first)
        cap(1, *second)
        finish(1, *first)
        store(1, *first)
        cap(1, *third)
        finish(1, *second)
        store(1, *second)
        finish(1, *third)
        store(1, *third)
